import numpy as np, ml_dtypes
CORES = [36,164,52,180,100,228,116,244]
N = 8
import mx_ref
BF = ml_dtypes.bfloat16
def entries(a):
    return np.ascontiguousarray(a.T).reshape(-1)
def table(e):
    return np.ascontiguousarray(np.reshape(e, (-1, 16)).T).astype(np.int32)
def pick(q, e):
    c = np.concatenate([q[0].reshape(128, -1, 4), np.zeros((128, 1, 4), np.uint8)], axis=1); s = np.concatenate([q[1], np.ones((16, 1), np.uint8)], axis=1)
    return (np.ascontiguousarray(c[:, e].reshape(128, -1)), np.ascontiguousarray(s[:, e]))
def join(*qs):
    return (np.concatenate([q[0] for q in qs], axis=1), np.concatenate([q[1] for q in qs], axis=1))
def put(q, e, v):
    c, s = q[0].reshape(128, -1, 4).copy(), q[1].copy(); c[:, e] = v[0].reshape(128, -1, 4); s[:, e] = v[1]
    return (c.reshape(128, -1), s)
def pk(c, s):
    return (np.ascontiguousarray(c), mx_ref.live(s))
def emit(q):
    return q[0], q[1]
def cols(t, e):
    v = np.concatenate([t.reshape(128, -1, 4), np.zeros((128, 1, 4), BF)], axis=1)
    return np.ascontiguousarray(v[:, e]).reshape(128, -1)
def cut(t, i, w=512):
    return t[:, w * i:w * i + w]
def f(rng, *shape):
    return mx_ref.flush((rng.standard_normal(shape, dtype=np.float32) * np.exp2(rng.integers(-2, 3, shape[:-1] + (1,)))).astype(BF))
def wide(rng, *shape, cols=0):
    v = rng.standard_normal(shape, dtype=np.float32) * np.exp2(rng.integers(-12, 13, shape)).astype(np.float32)
    if cols: v *= np.repeat(np.exp2(rng.integers(-cols, cols + 1, shape[:-2] + (1, shape[-1] // 4))) * (rng.random(shape[:-2] + (1, shape[-1] // 4)) > 0.0625), 4, axis=-1).astype(np.float32)
    return mx_ref.flush(v.astype(BF))
P, CAPP, LC = 128, 16, 64
def choose(e, g, d):
    c = e[np.arange(P), np.argmax(g[e], axis=1)]
    for s in range(N):
        if s != d:
            late = np.flatnonzero(c // P == s)[CAPP:]
            c[late] = e[late, 0]
    return c
def play(e0, e1, e2, p1, p2, u, a):
    k = [mx_ref.quantize(u[d]) for d in range(N)]
    A = [[mx_ref.quantize(np.ascontiguousarray(cut(a[d], i))) for i in range(4)] for d in range(N)]
    H = [mx_ref.quantize(e0[d]) for d in range(N)]
    g = np.stack([mx_ref.matmul(k[d], H[d])[0] for d in range(N)]) + np.float32(0)
    chosen, tiles, scores = [], [], [g]
    for e, p in ((e1, p1), (e2, p2)):
        every, before = join(*H), g.reshape(-1)
        H, g = [], np.zeros((N, P), np.float32)
        for d in range(N):
            c = choose(entries(p[d]).reshape(P, 4), before, d)
            x = pick(every, c)
            R = np.stack([mx_ref.matmul(A[d][i], x) for i in range(4)], axis=2).reshape(128, 4 * P)
            h = (R * np.float32(0.05) + e[d].astype(np.float32)).astype(BF)
            q = mx_ref.quantize(h)
            g[d] = before[c] + mx_ref.matmul(k[d], q)[0]
            H.append(q)
            chosen.append(c)
            tiles.append(h)
        scores.append(g)
    return np.stack(chosen).reshape(2, N, P), tiles, scores, H
def large(v):
    v = v.astype(np.float32)
    v[np.abs(v) < np.float32(0.03125)] = 0
    return v.astype(BF)
def lean(v, u, s):
    t = np.abs(v.astype(np.float32)).reshape(128, -1, 4) * np.sign(u[:, None, :4].astype(np.float32)) * np.asarray(s, np.float32)[None, :, None]
    return t.reshape(128, -1).astype(BF)
def near(t, u, score):
    size = np.concatenate([[0.0], np.exp2(np.arange(-26, -7))])[:, None] * np.array([1, 1.25, 1.5, 1.75])
    v = np.repeat(t.astype(np.float32).reshape(128, 1, 4), 80, axis=1)
    v[:8] = np.sign(u[:8, None, :4].astype(np.float32)) * size.reshape(1, 80, 1)
    v = np.ascontiguousarray(v.reshape(128, 320).astype(BF))
    s = score(v)
    i = int(np.argmin(np.abs(s - s[0] - np.float32(2.5) * np.spacing(np.abs(s[0])))))
    return cols(v, [0, i])
def strong(u):
    return (u.astype(np.float32) * np.float32(2.0 ** 24)).astype(BF)
def lists(rng):
    out = []
    for d in range(N):
        others = np.delete(np.arange(N), d)
        rank = others[np.argsort(rng.random((P, N - 1)), axis=1)[:, :3]]
        pool = np.stack([rng.permutation(P)[:LC] for s in range(N)])
        e = np.zeros((P, 4), int)
        e[:, 0] = d * P + rng.integers(0, P, P)
        e[:, 1:] = rank * P + pool[rank, rng.integers(0, LC, (P, 3))]
        out.append(table(e.reshape(-1)))
    return np.stack(out)
def crowd(rng, s):
    out, half = [], LC // 2
    for d in range(N):
        x = rng.permutation(np.delete(np.arange(N), d))
        hi = np.stack([rng.permutation(np.flatnonzero(s[r]))[:half] for r in range(N)])
        lo = np.stack([rng.permutation(np.flatnonzero(~s[r]))[:half] for r in range(N)])
        j = rng.permutation(P)
        one, two, home = j[:P // 2], j[P // 2:P // 2 + CAPP], j[P // 2 + CAPP:]
        rank = np.stack([np.full(P, x[0]), np.full(P, x[1]), x[rng.integers(2, N - 1, P)]], axis=1)
        n = rng.integers(0, half, (P, 3))
        n[j, 0] = np.arange(P) % (P // 2) % half
        n[two, 1] = rng.permutation(half)[:CAPP]
        at = lo[rank, n]
        at[one, 0] = hi[x[0], n[one, 0]]
        at[two, 1] = hi[x[1], n[two, 1]]
        e = np.zeros((P, 4), int)
        e[:, 0] = d * P + np.flatnonzero(~s[d])[rng.integers(0, P // 2, P)]
        e[home, 0] = d * P + np.flatnonzero(s[d])[rng.integers(0, P // 2, home.size)]
        e[:, 1:] = rng.permuted(rank * P + at, axis=1)
        out.append(table(e.reshape(-1)))
    return np.stack(out)
def plain(rng):
    u = np.array(f(rng, 128, 512))
    u[:, 4:] = 0
    return {"e0": np.array(f(rng, N, 128, 4 * P)), "e1": large(f(rng, N, 128, 4 * P)), "e2": large(f(rng, N, 128, 4 * P)), "p1": lists(rng), "p2": lists(rng),
            "u": np.stack([u] * N), "a": f(rng, N, 128, 2048), "w": f(rng, N, 128, 512)}
def setup_inputs(rng):
    return plain(rng)
def setup_inputs_full(rng):
    d = plain(rng)
    for e, p, size in (("e0", "p1", 1), ("e1", "p2", 64)):
        s = np.stack([rng.permutation(P) < P // 2 for r in range(N)])
        for r in range(N): d[e][r] = lean(d[e][r], d["u"][r], size * np.where(s[r], 1, -1))
        d[p] = crowd(rng, s)
    return d
def setup_inputs_ties(rng):
    d = plain(rng)
    u, a = np.ascontiguousarray(d["u"][0]), np.array(d["a"][0])
    a.reshape(128, 4, 512)[:, :, :32] = 0
    k = mx_ref.quantize(u)
    def row(t): return mx_ref.matmul(k, mx_ref.quantize(t))[0]
    x = np.concatenate([f(rng, 128, 16), near(lean(f(rng, 128, 4), u, [1]), u, row)], axis=1)
    best = cols(x, [5] * 4)
    top, q = row(best)[0], mx_ref.quantize(best)
    R = np.stack([mx_ref.matmul(mx_ref.quantize(np.ascontiguousarray(cut(a, i))), q)[:, 0] for i in range(4)], axis=1)
    def later(t): return top + row((np.tile(R, 80) * np.float32(0.05) + t.astype(np.float32)).astype(BF))
    z = near(lean(large(f(rng, 128, 4)), u, [8]), u, later)
    d["e0"] = np.stack([cols(x, rng.integers(0, 6, P)) for r in range(N)])
    d["e1"] = np.stack([cols(z, rng.integers(0, 2, P)) for r in range(N)])
    d["a"] = np.stack([a] * N)
    return d
def setup_inputs_own(rng):
    d = plain(rng)
    d["u"] = strong(d["u"])
    best, worst = rng.permutation(N)[:2]
    for r, s in ((best, 1), (worst, -1)):
        d["e0"][r] = lean(d["e0"][r], d["u"][r], np.full(P, 8 * s))
        d["e1"][r] = lean(d["e1"][r], d["u"][r], np.full(P, 256 * s))
    return d
def setup_inputs_flip(rng):
    d = plain(rng)
    d["u"] = strong(d["u"])
    for r in range(N):
        s = rng.permutation(P) % 2 * 2 - 1
        d["e0"][r] = lean(d["e0"][r], d["u"][r], 1024 * s)
        d["e1"][r] = lean(d["e1"][r], d["u"][r], -16384 * s)
    return d
def setup_inputs_spread(rng):
    d = plain(rng)
    d["e0"] = wide(rng, N, 128, 4 * P, cols=4)
    d["e1"] = large(wide(rng, N, 128, 4 * P, cols=4))
    d["e2"] = large(wide(rng, N, 128, 4 * P, cols=4))
    return d
def check_inputs(d):
    b = []
    for k in ("e0", "e1", "e2", "u", "a", "w"):
        v = np.abs(d[k].astype(np.float32))
        if not (np.isfinite(v).all() and ((v == 0) | (v >= 2.0 ** -30) & (v <= 2.0 ** 30)).all()): b.append("a value of " + k)
    u = d["u"].astype(np.float32)
    if (u[:, :, 4:] != 0).any(): b.append("u has numbers behind its column 0")
    if (u != u[:1]).any(): b.append("u isn't the same on all ranks")
    for k in ("p1", "p2"):
        for r in range(N):
            e = entries(d[k][r]).reshape(P, 4)
            if e.min() < 0 or e.max() >= N * P:
                b.append(k + " out of range")
                continue
            o = np.sort(e[:, 1:] // P, axis=1)
            if (e[:, 0] // P != r).any(): b.append(k + ": predecessor 0")
            if (o == r).any() or (o[:, 1:] == o[:, :-1]).any(): b.append(k + ": predecessors 1 to 3")
            if np.bincount(np.unique(e[:, 1:]) // P, minlength=N).max() > LC: b.append(k + ": too many columns of one rank")
    if not b:
        chosen, tiles, scores, H = play(*[d[k] for k in ("e0", "e1", "e2", "p1", "p2", "u", "a")])
        v = np.abs(np.stack(tiles).astype(np.float32))
        if not (np.isfinite(v).all() and ((v == 0) | (v >= 2.0 ** -30) & (v <= 2.0 ** 30)).all()): b.append("a value of h_1 or h_2")
        if not np.isfinite(np.stack(scores)).all(): b.append("a score")
    return b
def reference(e0, e1, e2, p1, p2, u, a, w):
    chosen, tiles, scores, H = play(e0, e1, e2, p1, p2, u, a)
    ch, g = np.zeros((N, 2, P), np.float32), np.zeros((N, 1, P), np.float32)
    oc, osc, y = np.zeros((N, 128, 4 * P), np.uint8), np.zeros((N, 16, P), np.uint8), np.zeros((N, 128, P), np.float32)
    for r in range(N):
        ch[r] = chosen[:, r]
        g[r, 0] = scores[2][r]
        oc[r], osc[r] = emit(H[r])
        y[r] = mx_ref.matmul(mx_ref.quantize(w[r]), H[r])
    return {"ch": ch, "g": g, "oc": oc, "osc": osc, "y": y}

@@ -1,0 +1,311 @@
+from concourse.bass import DstId, RemoteDMATransfer, IndirectOffsetOnAxis
+from concourse.mybir import dt, AluOpType, ActivationFunctionType
+
+X4 = "float8_e4m3fn_x4"
+F, B, I, U16, U8 = "float32", "bfloat16", "int32", "uint16", "uint8"
+
+
+def _sb(n, d):
+    return ("sbuf", [128, n], d)
+
+
+SCRATCH = {
+    "e0t": _sb(512, B), "e1t": _sb(512, B), "e2t": _sb(512, B), "at": _sb(2048, B), "wt": _sb(512, B), "ut": _sb(4, B),
+    "ubig": _sb(512, B),
+    "pst": ("dram", [128, 4], I), "pl": ("dram", [8, 128, 4], I),
+    "l1": _sb(32, I), "l2": _sb(32, I),
+    "uq": _sb(128, X4), "us": _sb(128, U8), "aq": _sb(512, X4), "asc": _sb(512, U8), "wq": _sb(128, X4), "ws": _sb(128, U8),
+    "hall": _sb(1024, X4), "halls": _sb(1024, U8), "x1": _sb(128, X4), "x1s": _sb(128, U8),
+    "h1q": _sb(128, X4), "h1s": _sb(128, U8), "pk": _sb(128, X4), "pks": _sb(128, U8),
+    "win2": _sb(256, X4), "win2s": _sb(256, U8), "x2": _sb(128, X4), "x2s": _sb(128, U8),
+    "h2q": _sb(128, X4), "h2s": _sb(128, U8),
+    "ones": _sb(128, B), "hold32": _sb(512, B), "hold16": _sb(128, B), "rst": _sb(512, F), "pidx": _sb(1, I), "ridx": _sb(1, I),
+    "r31": _sb(1, I), "ip": _sb(1, F), "sp31": _sb(1, F), "spx": _sb(1, F), "spart": _sb(1, F), "colmod": _sb(128, F),
+    "mask16": _sb(128, B), "repi": _sb(32, I), "repo": _sb(32, U16), "dupi": _sb(16, I), "dupo": _sb(16, U16),
+    "io1": _sb(1024, F), "eidx": _sb(512, F),
+    "off1": _sb(32, U16), "off2": _sb(32, U16), "er": _sb(512, F), "kt": _sb(512, F),
+    "key1": _sb(512, F), "key2": _sb(512, F), "e0r2": _sb(128, F), "e0b2": _sb(128, F), "ew": _sb(128, F), "es": _sb(128, F),
+    "sc": _sb(1024, F), "gv": _sb(512, F), "mx": _sb(512, F), "pm": _sb(512, B), "st": _sb(512, F),
+    "zi1": _sb(128, I), "zi2": _sb(128, I), "zb2": _sb(128, I),
+    "sj": _sb(128, I), "cj": _sb(128, I), "mk": _sb(128, B), "cw": _sb(128, F), "cum": _sb(128, B), "cs": _sb(128, F),
+    "vv": _sb(128, B), "v2": _sb(256, B), "vt": _sb(256, B), "vs": _sb(256, B), "ov": _sb(8, F), "df": _sb(8, F), "od": _sb(8, F),
+    "cf": _sb(8, F), "cu1": _sb(8, U16), "cu2": _sb(8, U16),
+    "base1": _sb(128, F), "grow": _sb(128, F), "gt": _sb(128, F), "sp": _sb(32, F), "d1": _sb(512, F), "rp": _sb(1024, F),
+    "sc2": _sb(1024, F), "base2": _sb(128, F), "gout": _sb(128, F), "yt": _sb(128, F),
+    "am": _sb(128, I), "mb": _sb(144, B), "ce": _sb(128, B), "pp": _sb(128, B), "ks": _sb(128, F), "lr": _sb(32, F),
+    "lt": _sb(32, F), "ls": _sb(32, F), "r8": _sb(8, F), "r8i": _sb(8, I), "r8n": _sb(8, I), "offp": _sb(8, U16),
+    "ti": _sb(8, I), "tsh": _sb(8, I), "t1": _sb(8, F), "t2": _sb(8, F), "isr": _sb(8, F), "isk": _sb(8, F), "own": _sb(8, F),
+    "dd": _sb(8, F), "de": _sb(8, F), "ix": _sb(8, F), "ixu": _sb(8, U16),
+    "chr1": _sb(128, F), "chr2": _sb(128, F),
+    "hs1": _sb(512, F), "hs2": _sb(512, F), "h1": _sb(512, B), "h2": _sb(512, B),
+    "ps": ("psum", [128, 2048], F), "pr": ("psum", [128, 2048], F),
+}
+
+REMOTE = ["al", "a0", "ae", "a2", "left"]
+SEMAPHORES = REMOTE + ["v"] + ["s%d" % i for i in range(130)]
+A = AluOpType
+CP = ActivationFunctionType.Copy
+TOP = 2.0 ** 19
+
+
+def rank_program(g, core, T, topo):
+    me = T.rank_of(core)
+    if me is None:
+        return
+    N = len(T.cores)
+    Q = {"g": g, "v": g.vector, "s": g.scalar, "t": g.tensor, "y": g.sync}
+    total, seen, used = {}, {}, [0]
+
+    def wait(q, deps):
+        for sem in deps:
+            assert sem != "v" or q == "v"
+            if seen.get((q, sem), 0) < total.get(sem, 0):
+                Q[q].wait_ge(T.sem[sem], total[sem])
+                seen[(q, sem)] = total[sem]
+
+    def fresh():
+        used[0] += 1
+        return "s%d" % (used[0] - 1)
+
+    def mark(q, ins, n, cross, sem=None):
+        if sem is None:
+            sem = "v" if q == "v" and not cross else fresh()
+        total[sem] = total.get(sem, 0) + n
+        ins.then_inc(T.sem[sem], n)
+        return sem
+
+    def dma(q, out, in_, deps=(), sem=None):
+        wait(q, deps)
+        return mark(q, Q[q].dma_start(out, in_), 16, True, sem)
+
+    F_ = {"copy": g.vector.tensor_copy, "tt": g.vector.tensor_tensor, "ts": g.vector.tensor_scalar, "set": g.vector.memset,
+          "scan": g.vector.tensor_tensor_scan, "tr": g.vector.transpose, "quant": g.vector.quantize_mx,
+          "mm": g.tensor.matmul_mx, "act": g.scalar.activation, "iota": g.iota, "bc": g.partition_broadcast}
+
+    def op(q, name, args, deps=(), cross=True, sem=None, **kw):
+        wait(q, deps)
+        return mark(q, F_[name](*args, **kw), 1, cross, sem)
+
+    def v(name, *args, deps=("v",), cross=False):
+        return op("v", name, args, deps, cross)
+
+    def send(sem, src, dst, deps):
+        wait("g", deps)
+        tr = []
+        for q in range(1, N):
+            d = (me + q) % N
+            c = T.cores[d]
+            rid, pid = topo.addr(c, core)
+            e = topo.engines(core, c)
+            tr.append(RemoteDMATransfer(dst_ids=[DstId(rid=rid, pnc=pid)], dma_engine_mask=1 << e[q % len(e)],
+                                        remote_sem=T.sem[sem], srcs=[src(q)], dsts=[dst(d)]))
+        g.remote_dma_fused(tr, local_sem=T.sem.left)
+        total["left"] = total.get("left", 0) + N - 1
+
+    total["al"], total["ae"] = N - 1, N - 1
+    total["a0"], total["a2"] = 2 * (N - 1), 2 * (N - 1)
+    mine = slice(128 * me, 128 * me + 128)
+
+    ld_e0 = dma("y", T.e0t[:], T.e0[:])
+    ld_ps = dma("s", T.pst[:], T.p2[:])
+    ld_u = dma("s", T.ut[:], T.u[:, 0:4])
+    ld_own = dma("s", T.pl[0], T.p2[:])
+    ld_a = dma("y", T.at[:], T.a[:])
+    ld_e1 = dma("y", T.e1t[:], T.e1[:])
+    ld_w = dma("y", T.wt[:], T.w[:])
+    ld_e2 = dma("y", T.e2t[:], T.e2[:])
+
+    def iota(out, pattern, base=0, cm=0, fl=False):
+        if fl:
+            return op("g", "iota", (out, pattern, base, cm), allow_small_or_imprecise_dtypes=True)
+        return op("g", "iota", (out, pattern, base, cm))
+
+    i_p = iota(T.pidx[:], [[0, 1]], 0, 1)
+    i_1 = iota(T.io1[:], [[1, 1024]], 0, 0, True)
+    v("set", T.ones[:], 1.0)
+    x_ridx = v("ts", T.ridx[:], T.pidx[:], 15, None, A.bitwise_and, deps=(i_p,), cross=True)
+
+    send("al", lambda q: T.pst[:], lambda d: T.pl[(me - d) % N], (ld_ps,))
+    x_h0 = v("quant", T.hall[:, mine], T.halls[:, mine], T.e0t[:], deps=(ld_e0,), cross=True)
+    send("a0", lambda q: T.hall[:, mine].bitcast(dt.uint8), lambda d: T.hall[:, mine].bitcast(dt.uint8), (x_h0,))
+    send("a0", lambda q: T.halls[:, mine], lambda d: T.halls[:, mine], (x_h0,))
+
+    wait("g", (x_ridx,))
+    ld_l1 = mark("g", g.indirect_dma_start(T.l1[:], None, T.p1[:], IndirectOffsetOnAxis(ap=T.ridx[:], axis=0), bounds_check=15), 16, True)
+    i_e = iota(T.eidx[:], [[1024, 512]], 0, 0, True)
+    i_c = iota(T.colmod[:], [[0, 8], [1, 16]], 0, 0, True)
+    i_r = iota(T.repi[:], [[1, 16], [0, 2]], 16, 0)
+    i_d = iota(T.dupi[:], [[16, 8], [0, 2]], 0, 0)
+    ld_l2 = dma("y", T.l2[:], T.pl[:], ("al", ld_own))
+
+    for t in range(4):
+        v("ts", T.ubig[:, t:512:4], T.ones[:], T.ut[:, t:t + 1], None, A.mult, deps=("v", ld_u))
+    x_u = v("quant", T.uq[:], T.us[:], T.ubig[:], cross=True)
+    for buf, c in ((T.hold32[:], 1.0), (T.hold16[:], 1.0), (T.rst[:], 0.0), (T.pm[:, 0:512:4], 1.0), (T.mb[:, 0:1], 0.0), (T.d1[:], 0.0)):
+        v("set", buf, c, deps=())
+    v("copy", T.ip[:], T.ridx[:], deps=(x_ridx,))
+    v("ts", T.r31[:], T.pidx[:], 31, None, A.bitwise_and, deps=())
+    v("set", T.hold32[:, 0:512:32], 0.0)
+    v("set", T.hold16[:, 0:128:16], 0.0, deps=())
+    v("set", T.rst[:, 0:512:4], -1.0e29, deps=())
+    v("copy", T.sp31[:], T.r31[:], deps=())
+    v("ts", T.spx[:], T.sp31[:], float(me), 99.0, A.is_equal, A.mult)
+    v("tt", T.spart[:], T.spx[:], T.sp31[:], A.add)
+    v("ts", T.mask16[:], T.colmod[:], T.ip[:], None, A.is_equal, deps=(i_c,))
+    x_rep = v("copy", T.repo[:], T.repi[:], deps=(i_r,), cross=True)
+    v("ts", T.dupo[:], T.dupi[:], T.ip[:], None, A.add, deps=(i_d,))
+
+    def prep(off, key, ld, lt):
+        v("copy", off[:], lt[:], deps=(ld,))
+        v("copy", T.er[:], T.io1[:].indirect(off[:]), deps=("v", i_1))
+        v("tt", T.kt[:], T.er[:], T.eidx[:], A.add, deps=("v", i_e))
+        v("ts", key[:], T.kt[:], 1.0 / TOP, None, A.mult)
+
+    def e0table(row, deps):
+        v("tt", T.ew[:], row, T.mask16[:], A.mult, deps=deps)
+        v("scan", T.es[:], T.hold16[:], T.ew[:], 0.0, A.mult, A.add)
+
+    prep(T.off1, T.key1, ld_l1, T.l1)
+    e0table(T.er[:, 0:512:4], ("v",))
+    x_a = v("quant", T.aq[:], T.asc[:], T.at[:], deps=(ld_a,), cross=True)
+    prep(T.off2, T.key2, ld_l2, T.l2)
+    x_e0r = v("copy", T.e0r2[:], T.er[:, 0:512:4], cross=True)
+    b_e0 = op("g", "bc", (T.e0b2[:], T.e0r2[0:1, :], 128), (x_e0r,))
+    x_w = v("quant", T.wq[:], T.ws[:], T.wt[:], deps=(ld_w,), cross=True)
+
+    sc_done = []
+    for b in range(4):
+        cs = slice(256 * b, 256 * b + 256)
+        m = op("t", "mm", (T.ps[:, 512 * b:512 * b + 256], T.uq[:], T.us[:], T.hall[:, cs], T.halls[:, cs], True, True), (x_u, x_h0, "a0"))
+        if b % 2 == 0:
+            v("copy", T.sc[:, cs], T.ps[:, 512 * b:512 * b + 256], deps=(m,))
+        else:
+            sc_done.append(op("s", "act", (T.sc[:, cs], T.ps[:, 512 * b:512 * b + 256], CP), (m,)))
+
+    def choose(win, off, key, deps):
+        v("copy", T.gv[:], win[:].indirect(off[:]), deps=["v"] + deps)
+        v("scan", T.mx[:], T.rst[:], T.gv[:], 0.0, A.add, A.max)
+        for k in (1, 2, 3):
+            v("tt", T.pm[:, k:512:4], T.gv[:, k:512:4], T.mx[:, k - 1:512:4], A.is_gt, deps=("v",) if k == 1 else ())
+        v("scan", T.st[:], T.pm[:], key[:], 0.0, A.max, A.min)
+
+    def capacity(zi, deps):
+        v("ts", T.sj[:], zi, 7, 7, A.logical_shift_right, A.bitwise_and, deps=deps)
+        v("ts", T.cj[:], zi, 1023, None, A.bitwise_and, deps=())
+        v("ts", T.mk[:], T.sj[:], T.spart[:], None, A.is_equal)
+        v("scan", T.cum[:], T.ones[:], T.mk[:], 0.0, A.mult, A.add)
+        v("tt", T.cw[:], T.cj[:], T.mask16[:], A.mult, deps=())
+        v("tt", T.vv[:], T.mk[:], T.cum[:], A.mult)
+        v("scan", T.cs[:], T.hold16[:], T.cw[:], 0.0, A.mult, A.add, deps=())
+        v("copy", T.v2[:], T.vv[:].indirect(T.dupo[:]))
+        v("tr", T.vt[:], T.v2[:])
+        v("tt", T.df[:], T.es[:, 15:128:16], T.cs[:, 15:128:16], A.subtract, deps=())
+        v("scan", T.vs[:], T.hold32[:, 0:256], T.vt[:], 0.0, A.mult, A.add)
+        v("ts", T.ov[:], T.vs[:, 31:256:32], 16.5, None, A.is_gt)
+        v("tt", T.od[:], T.ov[:], T.df[:], A.mult)
+        v("tt", T.cf[:], T.od[:], T.cs[:, 15:128:16], A.add)
+
+    def update(hs, h, X, Xs, e, ld_e, deps, between):
+        dep = []
+        for i in range(4):
+            s = slice(128 * i, 128 * i + 128)
+            m = op("t", "mm", (T.pr[:, 512 * i:512 * i + 128], T.aq[:, s], T.asc[:, s], X[:], Xs[:], True, True), deps)
+            dep.append(op("s", "act", (hs[:, s], T.pr[:, 512 * i:512 * i + 128], CP), (m,), scale=0.05))
+        between()
+        for i in range(4):
+            v("tt", h[:, i:512:4], hs[:, 128 * i:128 * i + 128], e[:, i:512:4], A.add, deps=(dep[i], ld_e))
+
+    choose(T.sc, T.off1, T.key1, sc_done)
+    v("ts", T.zi1[:], T.st[:, 3:512:4], TOP, None, A.mult)
+    capacity(T.zi1[:], ("v",))
+    x_c1 = v("copy", T.cu1[:], T.cf[:], cross=True)
+    s_x1 = op("s", "act", (T.x1s[:], T.halls[:].indirect(T.cu1[:]), CP), (x_c1, "a0", x_h0))
+    x_x1 = v("copy", T.x1[:].bitcast(dt.uint32), T.hall[:].bitcast(dt.uint32).indirect(T.cu1[:]), deps=(x_c1, "a0", x_h0), cross=True)
+    cross1 = []
+
+    def between1():
+        v("copy", T.base1[:], T.sc[:].indirect(T.cu1[:]), deps=("v", x_c1))
+        cross1.append(v("copy", T.chr1[:], T.io1[:].indirect(T.cu1[:]), deps=(), cross=True))
+
+    update(T.hs1, T.h1, T.x1, T.x1s, T.e1t, ld_e1, (x_x1, s_x1, x_a), between1)
+    dma("y", T.ch[0:1, :], T.chr1[0:1, :], (cross1[0],))
+    x_h1 = v("quant", T.h1q[:], T.h1s[:], T.h1[:], cross=True)
+
+    m = op("t", "mm", (T.ps[:, 0:128], T.uq[:], T.us[:], T.h1q[:], T.h1s[:], True, True), (x_h1,))
+    v("quant", T.win2[:, 128:256], T.win2s[:, 128:256], T.h1[:], deps=())
+    v("tt", T.grow[:], T.ps[:, 0:128], T.base1[:], A.add, deps=(m, "v"))
+    v("tr", T.gt[:], T.grow[:])
+    x_sp = v("copy", T.sp[:, 4 * me:4 * me + 4], T.gt[:, 0:128:32], cross=True)
+    send("ae", lambda q: T.sp[:, 4 * me:4 * me + 4], lambda d: T.sp[:, 4 * me:4 * me + 4], (x_sp,))
+    e0table(T.e0b2[:], ("v", b_e0))
+
+    v("copy", T.d1[:, 0:512:32], T.sp[:, 0:16], deps=("ae", x_sp))
+    s_rp = op("s", "act", (T.rp[:, 512:1024], T.sp[:].indirect(T.repo[:]), CP), ("ae", x_sp, x_rep))
+    v("scan", T.rp[:, 0:512], T.hold32[:], T.d1[:], 0.0, A.mult, A.add)
+    v("tr", T.sc2[:, 0:512], T.rp[:, 0:512])
+    v("tr", T.sc2[:, 512:1024], T.rp[:, 512:1024], deps=(s_rp,))
+
+    choose(T.sc2, T.off2, T.key2, [])
+    x_z2 = v("ts", T.zi2[:], T.st[:, 3:512:4], TOP, None, A.mult, cross=True)
+    b_z = op("g", "bc", (T.zb2[:], T.zi2[0:1, :], 128), (x_z2,))
+    v("ts", T.am[:], T.zi2[:], 896, None, A.bitwise_and, deps=(x_z2,))
+    v("ts", T.mb[:, 1:129], T.am[:], float(128 * me), None, A.is_equal)
+    v("scan", T.ce[:], T.ones[:], T.mb[:, 0:128], 0.0, A.mult, A.add)
+    v("ts", T.pp[:], T.ce[:], T.ip[:], None, A.is_le)
+    v("scan", T.ks[:], T.pp[:], T.st[:, 3:512:4], 0.0, A.max, A.min)
+    v("ts", T.lr[:], T.mask16[:, 0:32], T.ks[:, 127:128], None, A.mult)
+    v("tr", T.lt[:], T.lr[:])
+    x_ls = v("scan", T.ls[:], T.hold16[:, 0:32], T.lt[:], 0.0, A.mult, A.add, cross=True)
+    s_r8 = fresh()
+    for b in range(4):
+        for a in range(4):
+            o, i = T.r8[32 * b:32 * b + 32, 2 * a:2 * a + 2], T.ls[32 * a:32 * a + 32, 15:32:16]
+            if b < 2:
+                v("copy", o, i, deps=(x_ls,))
+            else:
+                op("s", "act", (o, i, CP), (x_ls,), sem=s_r8)
+    v("ts", T.r8i[:], T.r8[:], TOP, None, A.mult, deps=("v", s_r8))
+    v("ts", T.r8n[:], T.r8i[:], 127, None, A.bitwise_and)
+    x_of = v("copy", T.offp[:], T.r8n[:], cross=True)
+    s_pk = op("s", "act", (T.pks[:], T.h1s[:].indirect(T.offp[:]), CP), (x_of, x_h1))
+    x_pk = v("copy", T.pk[:].bitcast(dt.uint32), T.h1q[:].bitcast(dt.uint32).indirect(T.offp[:]), deps=(x_of, x_h1), cross=True)
+    land = slice(16 * me, 16 * me + 16)
+    send("a2", lambda q: T.pk[:, 16 * q:16 * q + 16].bitcast(dt.uint8), lambda d: T.win2[:, land].bitcast(dt.uint8), (x_pk,))
+    send("a2", lambda q: T.pks[:, 16 * q:16 * q + 16], lambda d: T.win2s[:, land], (s_pk,))
+
+    capacity(T.zb2[:], (b_z,))
+    x_c2 = v("copy", T.cu2[:], T.cf[:], cross=True)
+    cnt, ctab = T.vs[:, 31:256:32], T.cs[:, 15:128:16]
+    v("copy", T.ti[:], ctab, deps=())
+    v("ts", T.isr[:], cnt, 0.5, None, A.is_gt, deps=())
+    v("ts", T.own[:], T.cf[:], float(128 - 128 * me), None, A.add, deps=())
+    v("ts", T.tsh[:], T.ti[:], 7, None, A.logical_shift_right)
+    v("tt", T.isk[:], T.isr[:], T.ov[:], A.subtract, deps=())
+    v("ts", T.t1[:], T.tsh[:], 16.0, -1.0, A.mult, A.add)
+    v("tt", T.t2[:], T.t1[:], cnt, A.add)
+    v("tt", T.dd[:], T.t2[:], T.own[:], A.subtract)
+    v("tt", T.de[:], T.dd[:], T.isk[:], A.mult)
+    v("tt", T.ix[:], T.de[:], T.own[:], A.add)
+    x_ix = v("copy", T.ixu[:], T.ix[:], cross=True)
+    v("copy", T.base2[:], T.sc2[:].indirect(T.cu2[:]), deps=("v", x_c2))
+    x_ch2 = v("copy", T.chr2[:], T.io1[:].indirect(T.cu2[:]), deps=(), cross=True)
+    dma("y", T.ch[1:2, :], T.chr2[0:1, :], (x_ch2,))
+    s_x2 = op("s", "act", (T.x2s[:], T.win2s[:].indirect(T.ixu[:]), CP), (x_ix, "a2"))
+    x_x2 = v("copy", T.x2[:].bitcast(dt.uint32), T.win2[:].bitcast(dt.uint32).indirect(T.ixu[:]), deps=(x_ix, "a2"), cross=True)
+    update(T.hs2, T.h2, T.x2, T.x2s, T.e2t, ld_e2, (x_x2, s_x2, x_a), lambda: None)
+    x_h2 = v("quant", T.h2q[:], T.h2s[:], T.h2[:], cross=True)
+
+    m_y = op("t", "mm", (T.ps[:, 512:640], T.wq[:], T.ws[:], T.h2q[:], T.h2s[:], True, True), (x_h2, x_w))
+    m_g = op("t", "mm", (T.ps[:, 0:128], T.uq[:], T.us[:], T.h2q[:], T.h2s[:], True, True), (x_h2,))
+    s_y = op("s", "act", (T.yt[:], T.ps[:, 512:640], CP), (m_y,))
+    x_g = v("tt", T.gout[:], T.ps[:, 0:128], T.base2[:], A.add, deps=("v", m_g), cross=True)
+    dma("y", T.oc[:], T.h2q[:].bitcast(dt.uint8), (x_h2,))
+    for k in range(4):
+        dma("y", T.osc[4 * k:4 * k + 4, :], T.h2s[32 * k:32 * k + 4, :], (x_h2,))
+    dma("s", T.y[:], T.yt[:], (s_y,))
+    dma("y", T["g"][:], T.gout[0:1, :], (x_g,))
+
+    wait("v", ("v",))
+    for sem in sorted(total):
+        if sem != "v" and not any(seen.get((q, sem), 0) == total[sem] for q in Q):
+            wait("g", (sem,))

@@ -23,14 +23,14 @@ SCRATCH = {
     "r31": _sb(1, I), "ip": _sb(1, F), "sp31": _sb(1, F), "spx": _sb(1, F), "spart": _sb(1, F), "colmod": _sb(128, F),
     "mask16": _sb(128, B), "repi": _sb(32, I), "repo": _sb(32, U16), "dupi": _sb(16, I), "dupo": _sb(16, U16),
     "io1": _sb(1024, F), "eidx": _sb(512, F),
-    "off1": _sb(32, U16), "off2": _sb(32, U16), "er": _sb(512, F), "kt": _sb(512, F),
-    "key1": _sb(512, F), "key2": _sb(512, F), "e0r2": _sb(128, F), "e0b2": _sb(128, F), "ew": _sb(128, F), "es": _sb(128, F),
+    "off1": _sb(32, U16), "offq": _sb(8, U16), "off2": _sb(32, U16), "er": _sb(512, F), "kt": _sb(512, F),
+    "key1": _sb(128, F), "key2": _sb(512, F), "e0r2": _sb(128, F), "e0b2": _sb(128, F), "ew": _sb(128, F), "es": _sb(128, F),
     "sc": _sb(1024, F), "gv": _sb(512, F), "mx": _sb(512, F), "pm": _sb(512, B), "st": _sb(512, F),
-    "zi1": _sb(128, I), "zi2": _sb(128, I), "zb2": _sb(128, I),
+    "zrow": _sb(128, F), "zi1": _sb(128, I), "zi2": _sb(128, I), "zb2": _sb(128, I),
     "sj": _sb(128, I), "cj": _sb(128, I), "mk": _sb(128, B), "cw": _sb(128, F), "cum": _sb(128, B), "cs": _sb(128, F),
     "vv": _sb(128, B), "v2": _sb(256, B), "vt": _sb(256, B), "vs": _sb(256, B), "ov": _sb(8, F), "df": _sb(8, F), "od": _sb(8, F),
     "cf": _sb(8, F), "cu1": _sb(8, U16), "cu2": _sb(8, U16),
-    "base1": _sb(128, F), "grow": _sb(128, F), "gt": _sb(128, F), "sp": _sb(32, F), "d1": _sb(512, F), "rp": _sb(1024, F),
+    "base1": _sb(128, F), "bt": _sb(128, F), "gt": _sb(128, F), "sp": _sb(32, F), "d1": _sb(512, F), "rp": _sb(1024, F),
     "sc2": _sb(1024, F), "base2": _sb(128, F), "gout": _sb(128, F), "yt": _sb(128, F),
     "am": _sb(128, I), "mb": _sb(144, B), "ce": _sb(128, B), "pp": _sb(128, B), "ks": _sb(128, F), "lr": _sb(32, F),
     "lt": _sb(32, F), "ls": _sb(32, F), "r8": _sb(8, F), "r8i": _sb(8, I), "r8n": _sb(8, I), "offp": _sb(8, U16),
@@ -41,11 +41,12 @@ SCRATCH = {
     "ps": ("psum", [128, 2048], F), "pr": ("psum", [128, 2048], F),
 }
 
-REMOTE = ["al", "a0", "ae", "a2", "left"]
+REMOTE = ["al", "a0a", "a0b", "a0c", "ae", "a2", "left"]
 SEMAPHORES = REMOTE + ["v"] + ["s%d" % i for i in range(130)]
 A = AluOpType
 CP = ActivationFunctionType.Copy
 TOP = 2.0 ** 19
+TIERS = (("a0a", (1, 2, 3, 4), 2), ("a0b", (5, 6), 4), ("a0c", (7,), 8))
 
 
 def rank_program(g, core, T, topo):
@@ -89,21 +90,22 @@ def rank_program(g, core, T, topo):
     def v(name, *args, deps=("v",), cross=False):
         return op("v", name, args, deps, cross)
 
-    def send(sem, src, dst, deps):
+    def send(sem, src, dst, deps, qs=range(1, N), n=1):
         wait("g", deps)
         tr = []
-        for q in range(1, N):
+        for i, q in enumerate(qs):
             d = (me + q) % N
             c = T.cores[d]
             rid, pid = topo.addr(c, core)
             e = topo.engines(core, c)
-            tr.append(RemoteDMATransfer(dst_ids=[DstId(rid=rid, pnc=pid)], dma_engine_mask=1 << e[q % len(e)],
+            tr.append(RemoteDMATransfer(dst_ids=[DstId(rid=rid, pnc=pid)], dma_engine_mask=sum(1 << x for x in e[i * n:i * n + n]),
                                         remote_sem=T.sem[sem], srcs=[src(q)], dsts=[dst(d)]))
         g.remote_dma_fused(tr, local_sem=T.sem.left)
-        total["left"] = total.get("left", 0) + N - 1
+        total["left"] = total.get("left", 0) + n * len(tr)
 
-    total["al"], total["ae"] = N - 1, N - 1
-    total["a0"], total["a2"] = 2 * (N - 1), 2 * (N - 1)
+    total["al"], total["ae"], total["a2"] = N - 1, N - 1, 2 * (N - 1)
+    for sem, qs, n in TIERS:
+        total[sem] = 2 * n * len(qs)
     mine = slice(128 * me, 128 * me + 128)
 
     ld_e0 = dma("y", T.e0t[:], T.e0[:])
@@ -127,8 +129,9 @@ def rank_program(g, core, T, topo):
 
     send("al", lambda q: T.pst[:], lambda d: T.pl[(me - d) % N], (ld_ps,))
     x_h0 = v("quant", T.hall[:, mine], T.halls[:, mine], T.e0t[:], deps=(ld_e0,), cross=True)
-    send("a0", lambda q: T.hall[:, mine].bitcast(dt.uint8), lambda d: T.hall[:, mine].bitcast(dt.uint8), (x_h0,))
-    send("a0", lambda q: T.halls[:, mine], lambda d: T.halls[:, mine], (x_h0,))
+    for sem, qs, n in TIERS:
+        send(sem, lambda q: T.hall[:, mine].bitcast(dt.uint8), lambda d: T.hall[:, mine].bitcast(dt.uint8), (x_h0,), qs, n)
+        send(sem, lambda q: T.halls[:, mine], lambda d: T.halls[:, mine], (x_h0,), qs, n)
 
     wait("g", (x_ridx,))
     ld_l1 = mark("g", g.indirect_dma_start(T.l1[:], None, T.p1[:], IndirectOffsetOnAxis(ap=T.ridx[:], axis=0), bounds_check=15), 16, True)
@@ -155,39 +158,54 @@ def rank_program(g, core, T, topo):
     x_rep = v("copy", T.repo[:], T.repi[:], deps=(i_r,), cross=True)
     v("ts", T.dupo[:], T.dupi[:], T.ip[:], None, A.add, deps=(i_d,))
 
-    def prep(off, key, ld, lt):
-        v("copy", off[:], lt[:], deps=(ld,))
-        v("copy", T.er[:], T.io1[:].indirect(off[:]), deps=("v", i_1))
-        v("tt", T.kt[:], T.er[:], T.eidx[:], A.add, deps=("v", i_e))
-        v("ts", key[:], T.kt[:], 1.0 / TOP, None, A.mult)
-
     def e0table(row, deps):
         v("tt", T.ew[:], row, T.mask16[:], A.mult, deps=deps)
         v("scan", T.es[:], T.hold16[:], T.ew[:], 0.0, A.mult, A.add)
 
-    prep(T.off1, T.key1, ld_l1, T.l1)
-    e0table(T.er[:, 0:512:4], ("v",))
+    v("copy", T.off1[:], T.l1[:], deps=(ld_l1,))
+    for a in range(4):
+        v("copy", T.offq[32 * a:32 * a + 32, :], T.l1[32 * a:32 * a + 32, 8 * a:8 * a + 8], deps=())
+    v("copy", T.gv[:, 0:128], T.io1[:].indirect(T.offq[:]), deps=("v", i_1))
+    v("copy", T.er[:], T.io1[:].indirect(T.off1[:]), deps=())
+    v("tt", T.kt[:, 0:128], T.gv[:, 0:128], T.eidx[:, 0:128], A.add, deps=("v", i_e))
+    e0table(T.er[:, 0:512:4], ())
+    v("ts", T.key1[:], T.kt[:, 0:128], 1.0 / TOP, None, A.mult)
     x_a = v("quant", T.aq[:], T.asc[:], T.at[:], deps=(ld_a,), cross=True)
-    prep(T.off2, T.key2, ld_l2, T.l2)
+    v("copy", T.off2[:], T.l2[:], deps=(ld_l2,))
+    v("copy", T.er[:], T.io1[:].indirect(T.off2[:]))
+    v("tt", T.kt[:], T.er[:], T.eidx[:], A.add)
+    v("ts", T.key2[:], T.kt[:], 1.0 / TOP, None, A.mult)
     x_e0r = v("copy", T.e0r2[:], T.er[:, 0:512:4], cross=True)
     b_e0 = op("g", "bc", (T.e0b2[:], T.e0r2[0:1, :], 128), (x_e0r,))
     x_w = v("quant", T.wq[:], T.ws[:], T.wt[:], deps=(ld_w,), cross=True)
 
     sc_done = []
-    for b in range(4):
-        cs = slice(256 * b, 256 * b + 256)
-        m = op("t", "mm", (T.ps[:, 512 * b:512 * b + 256], T.uq[:], T.us[:], T.hall[:, cs], T.halls[:, cs], True, True), (x_u, x_h0, "a0"))
-        if b % 2 == 0:
-            v("copy", T.sc[:, cs], T.ps[:, 512 * b:512 * b + 256], deps=(m,))
+    order = [(me, x_h0)] + [((me - q) % N, sem) for sem, qs, n in TIERS for q in qs]
+    for i, (r, sem) in enumerate(order):
+        cs = slice(128 * r, 128 * r + 128)
+        bank = (T.ps if i < 4 else T.pr)[:, 512 * (i % 4):512 * (i % 4) + 128]
+        m = op("t", "mm", (bank, T.uq[:], T.us[:], T.hall[:, cs], T.halls[:, cs], True, True), (x_u, sem))
+        if i % 2:
+            v("copy", T.sc[:, cs], bank, deps=(m,))
         else:
-            sc_done.append(op("s", "act", (T.sc[:, cs], T.ps[:, 512 * b:512 * b + 256], CP), (m,)))
+            sc_done.append(op("s", "act", (T.sc[:, cs], bank, CP), (m,)))
+    arrived = [x_h0] + [sem for sem, qs, n in TIERS]
 
-    def choose(win, off, key, deps):
-        v("copy", T.gv[:], win[:].indirect(off[:]), deps=["v"] + deps)
-        v("scan", T.mx[:], T.rst[:], T.gv[:], 0.0, A.add, A.max)
+    def choose(w, key):
+        v("scan", T.mx[:, 0:w], T.rst[:, 0:w], T.gv[:, 0:w], 0.0, A.add, A.max)
         for k in (1, 2, 3):
-            v("tt", T.pm[:, k:512:4], T.gv[:, k:512:4], T.mx[:, k - 1:512:4], A.is_gt, deps=("v",) if k == 1 else ())
-        v("scan", T.st[:], T.pm[:], key[:], 0.0, A.max, A.min)
+            v("tt", T.pm[:, k:w:4], T.gv[:, k:w:4], T.mx[:, k - 1:w:4], A.is_gt, deps=("v",) if k == 1 else ())
+        return v("scan", T.st[:, 0:w], T.pm[:, 0:w], key[:], 0.0, A.max, A.min, cross=True)
+
+    def quarters(out, src, x):
+        sem = fresh()
+        for b in range(4):
+            for a in range(4):
+                if b < 2:
+                    v("copy", out(a, b), src(a), deps=(x,))
+                else:
+                    op("s", "act", (out(a, b), src(a), CP), (x,), sem=sem)
+        return sem
 
     def capacity(zi, deps):
         v("ts", T.sj[:], zi, 7, 7, A.logical_shift_right, A.bitwise_and, deps=deps)
@@ -215,17 +233,20 @@ def rank_program(g, core, T, topo):
         for i in range(4):
             v("tt", h[:, i:512:4], hs[:, 128 * i:128 * i + 128], e[:, i:512:4], A.add, deps=(dep[i], ld_e))
 
-    choose(T.sc, T.off1, T.key1, sc_done)
-    v("ts", T.zi1[:], T.st[:, 3:512:4], TOP, None, A.mult)
+    v("copy", T.gv[:, 0:128], T.sc[:].indirect(T.offq[:]), deps=["v"] + sc_done)
+    x_st = choose(128, T.key1)
+    s_z = quarters(lambda a, b: T.zrow[32 * b:32 * b + 32, 32 * a:32 * a + 32], lambda a: T.st[32 * a:32 * a + 32, 3:128:4], x_st)
+    v("ts", T.zi1[:], T.zrow[:], TOP, None, A.mult, deps=("v", s_z))
     capacity(T.zi1[:], ("v",))
     x_c1 = v("copy", T.cu1[:], T.cf[:], cross=True)
-    s_x1 = op("s", "act", (T.x1s[:], T.halls[:].indirect(T.cu1[:]), CP), (x_c1, "a0", x_h0))
-    x_x1 = v("copy", T.x1[:].bitcast(dt.uint32), T.hall[:].bitcast(dt.uint32).indirect(T.cu1[:]), deps=(x_c1, "a0", x_h0), cross=True)
+    s_x1 = op("s", "act", (T.x1s[:], T.halls[:].indirect(T.cu1[:]), CP), [x_c1] + arrived)
+    x_x1 = v("copy", T.x1[:].bitcast(dt.uint32), T.hall[:].bitcast(dt.uint32).indirect(T.cu1[:]), deps=[x_c1] + arrived, cross=True)
     cross1 = []
 
     def between1():
         v("copy", T.base1[:], T.sc[:].indirect(T.cu1[:]), deps=("v", x_c1))
         cross1.append(v("copy", T.chr1[:], T.io1[:].indirect(T.cu1[:]), deps=(), cross=True))
+        v("tr", T.bt[:], T.base1[:])
 
     update(T.hs1, T.h1, T.x1, T.x1s, T.e1t, ld_e1, (x_x1, s_x1, x_a), between1)
     dma("y", T.ch[0:1, :], T.chr1[0:1, :], (cross1[0],))
@@ -233,9 +254,8 @@ def rank_program(g, core, T, topo):
 
     m = op("t", "mm", (T.ps[:, 0:128], T.uq[:], T.us[:], T.h1q[:], T.h1s[:], True, True), (x_h1,))
     v("quant", T.win2[:, 128:256], T.win2s[:, 128:256], T.h1[:], deps=())
-    v("tt", T.grow[:], T.ps[:, 0:128], T.base1[:], A.add, deps=(m, "v"))
-    v("tr", T.gt[:], T.grow[:])
-    x_sp = v("copy", T.sp[:, 4 * me:4 * me + 4], T.gt[:, 0:128:32], cross=True)
+    v("tr", T.gt[:], T.ps[:, 0:128], deps=(m,))
+    x_sp = v("tt", T.sp[:, 4 * me:4 * me + 4], T.gt[:, 0:128:32], T.bt[:, 0:128:32], A.add, cross=True)
     send("ae", lambda q: T.sp[:, 4 * me:4 * me + 4], lambda d: T.sp[:, 4 * me:4 * me + 4], (x_sp,))
     e0table(T.e0b2[:], ("v", b_e0))
 
@@ -243,10 +263,13 @@ def rank_program(g, core, T, topo):
     s_rp = op("s", "act", (T.rp[:, 512:1024], T.sp[:].indirect(T.repo[:]), CP), ("ae", x_sp, x_rep))
     v("scan", T.rp[:, 0:512], T.hold32[:], T.d1[:], 0.0, A.mult, A.add)
     v("tr", T.sc2[:, 0:512], T.rp[:, 0:512])
-    v("tr", T.sc2[:, 512:1024], T.rp[:, 512:1024], deps=(s_rp,))
+    x_s2 = v("tr", T.sc2[:, 512:1024], T.rp[:, 512:1024], deps=(s_rp,), cross=True)
 
-    choose(T.sc2, T.off2, T.key2, [])
-    x_z2 = v("ts", T.zi2[:], T.st[:, 3:512:4], TOP, None, A.mult, cross=True)
+    s_g2 = op("s", "act", (T.gv[:, 256:512], T.sc2[:].indirect(T.off2[:, 16:32]), CP), (x_s2,))
+    v("copy", T.gv[:, 0:256], T.sc2[:].indirect(T.off2[:, 0:16]), deps=("v", x_s2))
+    wait("v", ("v", s_g2))
+    x_st2 = choose(512, T.key2)
+    x_z2 = v("ts", T.zi2[:], T.st[:, 3:512:4], TOP, None, A.mult, deps=(x_st2,), cross=True)
     b_z = op("g", "bc", (T.zb2[:], T.zi2[0:1, :], 128), (x_z2,))
     v("ts", T.am[:], T.zi2[:], 896, None, A.bitwise_and, deps=(x_z2,))
     v("ts", T.mb[:, 1:129], T.am[:], float(128 * me), None, A.is_equal)
@@ -256,14 +279,7 @@ def rank_program(g, core, T, topo):
     v("ts", T.lr[:], T.mask16[:, 0:32], T.ks[:, 127:128], None, A.mult)
     v("tr", T.lt[:], T.lr[:])
     x_ls = v("scan", T.ls[:], T.hold16[:, 0:32], T.lt[:], 0.0, A.mult, A.add, cross=True)
-    s_r8 = fresh()
-    for b in range(4):
-        for a in range(4):
-            o, i = T.r8[32 * b:32 * b + 32, 2 * a:2 * a + 2], T.ls[32 * a:32 * a + 32, 15:32:16]
-            if b < 2:
-                v("copy", o, i, deps=(x_ls,))
-            else:
-                op("s", "act", (o, i, CP), (x_ls,), sem=s_r8)
+    s_r8 = quarters(lambda a, b: T.r8[32 * b:32 * b + 32, 2 * a:2 * a + 2], lambda a: T.ls[32 * a:32 * a + 32, 15:32:16], x_ls)
     v("ts", T.r8i[:], T.r8[:], TOP, None, A.mult, deps=("v", s_r8))
     v("ts", T.r8n[:], T.r8i[:], 127, None, A.bitwise_and)
     x_of = v("copy", T.offp[:], T.r8n[:], cross=True)

@@ -1,4 +1,4 @@
-from concourse.bass import DstId, RemoteDMATransfer, IndirectOffsetOnAxis
+from concourse.bass import DstId, RemoteDMATransfer
 from concourse.mybir import dt, AluOpType, ActivationFunctionType
 
 X4 = "float8_e4m3fn_x4"
@@ -19,9 +19,9 @@ SCRATCH = {
     "h1q": _sb(128, X4), "h1s": _sb(128, U8), "pk": _sb(128, X4), "pks": _sb(128, U8),
     "win2": _sb(256, X4), "win2s": _sb(256, U8), "x2": _sb(128, X4), "x2s": _sb(128, U8),
     "h2q": _sb(128, X4), "h2s": _sb(128, U8),
-    "ones": _sb(128, B), "hold32": _sb(512, B), "hold16": _sb(128, B), "rst": _sb(512, F), "pidx": _sb(1, I), "ridx": _sb(1, I),
-    "r31": _sb(1, I), "ip": _sb(1, F), "sp31": _sb(1, F), "spx": _sb(1, F), "spart": _sb(1, F), "colmod": _sb(128, F),
-    "mask16": _sb(128, B), "repi": _sb(32, I), "repo": _sb(32, U16), "dupi": _sb(16, I), "dupo": _sb(16, U16),
+    "ones": _sb(128, B), "hold32": _sb(512, B), "hold16": _sb(128, B), "rst": _sb(512, F), "pidx": _sb(1, I), "r15": _sb(1, I),
+    "r31": _sb(1, I), "ip": _sb(1, F), "sp31": _sb(1, F), "spx": _sb(1, F), "spart": _sb(1, F), "cmod": _sb(128, I),
+    "mask16": _sb(128, B), "ci": _sb(128, I), "repo": _sb(32, U16), "rsh": _sb(32, I), "dupo": _sb(16, U16),
     "io1": _sb(1024, F), "eidx": _sb(512, F),
     "off1": _sb(32, U16), "offq": _sb(8, U16), "off2": _sb(32, U16), "er": _sb(512, F), "kt": _sb(512, F),
     "key1": _sb(128, F), "key2": _sb(512, F), "e0r2": _sb(128, F), "e0b2": _sb(128, F), "ew": _sb(128, F), "es": _sb(128, F),
@@ -111,21 +111,20 @@ def rank_program(g, core, T, topo):
     ld_e0 = dma("y", T.e0t[:], T.e0[:])
     ld_ps = dma("s", T.pst[:], T.p2[:])
     ld_u = dma("s", T.ut[:], T.u[:, 0:4])
+    ld_l1 = None
+    for k in range(8):
+        ld_l1 = dma("s", T.l1[16 * k:16 * k + 16, :], T.p1[:], (), ld_l1)
     ld_own = dma("s", T.pl[0], T.p2[:])
     ld_a = dma("y", T.at[:], T.a[:])
     ld_e1 = dma("y", T.e1t[:], T.e1[:])
     ld_w = dma("y", T.wt[:], T.w[:])
     ld_e2 = dma("y", T.e2t[:], T.e2[:])
 
-    def iota(out, pattern, base=0, cm=0, fl=False):
-        if fl:
-            return op("g", "iota", (out, pattern, base, cm), allow_small_or_imprecise_dtypes=True)
-        return op("g", "iota", (out, pattern, base, cm))
-
-    i_p = iota(T.pidx[:], [[0, 1]], 0, 1)
-    i_1 = iota(T.io1[:], [[1, 1024]], 0, 0, True)
+    i_p = op("g", "iota", (T.pidx[:], [[0, 1]], 0, 1))
+    i_1 = op("g", "iota", (T.io1[:], [[1, 1024]], 0, 0), allow_small_or_imprecise_dtypes=True)
     v("set", T.ones[:], 1.0)
-    x_ridx = v("ts", T.ridx[:], T.pidx[:], 15, None, A.bitwise_and, deps=(i_p,), cross=True)
+    v("ts", T.r15[:], T.pidx[:], 15, None, A.bitwise_and, deps=(i_p,))
+    v("ts", T.r31[:], T.pidx[:], 31, None, A.bitwise_and, deps=())
 
     send("al", lambda q: T.pst[:], lambda d: T.pl[(me - d) % N], (ld_ps,))
     x_h0 = v("quant", T.hall[:, mine], T.halls[:, mine], T.e0t[:], deps=(ld_e0,), cross=True)
@@ -133,51 +132,45 @@ def rank_program(g, core, T, topo):
         send(sem, lambda q: T.hall[:, mine].bitcast(dt.uint8), lambda d: T.hall[:, mine].bitcast(dt.uint8), (x_h0,), qs, n)
         send(sem, lambda q: T.halls[:, mine], lambda d: T.halls[:, mine], (x_h0,), qs, n)
 
-    wait("g", (x_ridx,))
-    ld_l1 = mark("g", g.indirect_dma_start(T.l1[:], None, T.p1[:], IndirectOffsetOnAxis(ap=T.ridx[:], axis=0), bounds_check=15), 16, True)
-    i_e = iota(T.eidx[:], [[1024, 512]], 0, 0, True)
-    i_c = iota(T.colmod[:], [[0, 8], [1, 16]], 0, 0, True)
-    i_r = iota(T.repi[:], [[1, 16], [0, 2]], 16, 0)
-    i_d = iota(T.dupi[:], [[16, 8], [0, 2]], 0, 0)
     ld_l2 = dma("y", T.l2[:], T.pl[:], ("al", ld_own))
+    s_e = op("s", "act", (T.eidx[:], T.io1[:, 0:512], CP), (i_1,), scale=1024.0 / TOP)
 
+    for a in range(4):
+        v("copy", T.offq[32 * a:32 * a + 32, :], T.l1[32 * a:32 * a + 32, 8 * a:8 * a + 8], deps=(ld_l1,))
+    v("copy", T.off1[:], T.l1[:], deps=())
     for t in range(4):
-        v("ts", T.ubig[:, t:512:4], T.ones[:], T.ut[:, t:t + 1], None, A.mult, deps=("v", ld_u))
-    x_u = v("quant", T.uq[:], T.us[:], T.ubig[:], cross=True)
-    for buf, c in ((T.hold32[:], 1.0), (T.hold16[:], 1.0), (T.rst[:], 0.0), (T.pm[:, 0:512:4], 1.0), (T.mb[:, 0:1], 0.0), (T.d1[:], 0.0)):
+        v("ts", T.ubig[:, t:512:4], T.ones[:], T.ut[:, t:t + 1], None, A.mult, deps=("v", ld_u) if t == 0 else ())
+    x_off1 = v("copy", T.ip[:], T.r15[:], cross=True)
+    s_gq = op("s", "act", (T.gv[:, 0:128], T.io1[:].indirect(T.offq[:]), CP), (x_off1, i_1), scale=1.0 / TOP)
+    s_er = op("s", "act", (T.er[:], T.io1[:].indirect(T.off1[:]), CP))
+    for buf, c in ((T.hold32[:], 1.0), (T.hold16[:], 1.0), (T.rst[:, 0:128], 0.0), (T.pm[:, 0:512:4], 1.0), (T.mb[:, 0:1], 0.0)):
         v("set", buf, c, deps=())
-    v("copy", T.ip[:], T.ridx[:], deps=(x_ridx,))
-    v("ts", T.r31[:], T.pidx[:], 31, None, A.bitwise_and, deps=())
-    v("set", T.hold32[:, 0:512:32], 0.0)
+    v("copy", T.ci[:], T.io1[:, 0:128], deps=(i_1,))
+    x_u = v("quant", T.uq[:], T.us[:], T.ubig[:], deps=("v",), cross=True)
+    v("set", T.hold32[:, 0:512:32], 0.0, deps=())
     v("set", T.hold16[:, 0:128:16], 0.0, deps=())
-    v("set", T.rst[:, 0:512:4], -1.0e29, deps=())
+    v("set", T.rst[:, 0:128:4], -1.0e29, deps=())
     v("copy", T.sp31[:], T.r31[:], deps=())
-    v("ts", T.spx[:], T.sp31[:], float(me), 99.0, A.is_equal, A.mult)
+    v("ts", T.cmod[:], T.ci[:], 15, None, A.bitwise_and, deps=())
+    v("ts", T.rsh[:], T.ci[:, 0:32], 1, None, A.logical_shift_right, deps=())
+    v("ts", T.spx[:], T.sp31[:], float(me), 99.0, A.is_equal, A.mult, deps=("v", x_off1))
+    v("ts", T.mask16[:], T.cmod[:], T.ip[:], None, A.is_equal, deps=())
+    v("ts", T.dupo[:], T.rsh[:, 0:16], 16.0, T.ip[:], A.mult, A.add, deps=())
+    x_rep = v("ts", T.repo[:], T.rsh[:], 16.0, None, A.add, deps=(), cross=True)
     v("tt", T.spart[:], T.spx[:], T.sp31[:], A.add)
-    v("ts", T.mask16[:], T.colmod[:], T.ip[:], None, A.is_equal, deps=(i_c,))
-    x_rep = v("copy", T.repo[:], T.repi[:], deps=(i_r,), cross=True)
-    v("ts", T.dupo[:], T.dupi[:], T.ip[:], None, A.add, deps=(i_d,))
+    v("tt", T.key1[:], T.gv[:, 0:128], T.eidx[:, 0:128], A.add, deps=(s_gq, s_e))
 
     def e0table(row, deps):
         v("tt", T.ew[:], row, T.mask16[:], A.mult, deps=deps)
         v("scan", T.es[:], T.hold16[:], T.ew[:], 0.0, A.mult, A.add)
 
-    v("copy", T.off1[:], T.l1[:], deps=(ld_l1,))
-    for a in range(4):
-        v("copy", T.offq[32 * a:32 * a + 32, :], T.l1[32 * a:32 * a + 32, 8 * a:8 * a + 8], deps=())
-    v("copy", T.gv[:, 0:128], T.io1[:].indirect(T.offq[:]), deps=("v", i_1))
-    v("copy", T.er[:], T.io1[:].indirect(T.off1[:]), deps=())
-    v("tt", T.kt[:, 0:128], T.gv[:, 0:128], T.eidx[:, 0:128], A.add, deps=("v", i_e))
-    e0table(T.er[:, 0:512:4], ())
-    v("ts", T.key1[:], T.kt[:, 0:128], 1.0 / TOP, None, A.mult)
+    e0table(T.er[:, 0:512:4], ("v", s_er))
     x_a = v("quant", T.aq[:], T.asc[:], T.at[:], deps=(ld_a,), cross=True)
-    v("copy", T.off2[:], T.l2[:], deps=(ld_l2,))
-    v("copy", T.er[:], T.io1[:].indirect(T.off2[:]))
-    v("tt", T.kt[:], T.er[:], T.eidx[:], A.add)
-    v("ts", T.key2[:], T.kt[:], 1.0 / TOP, None, A.mult)
-    x_e0r = v("copy", T.e0r2[:], T.er[:, 0:512:4], cross=True)
+    x_off2 = v("copy", T.off2[:], T.l2[:], deps=(ld_l2,), cross=True)
+    s_kt = op("s", "act", (T.kt[:], T.io1[:].indirect(T.off2[:]), CP), (x_off2,), scale=1.0 / TOP)
+    x_e0r = v("ts", T.e0r2[:], T.kt[:, 0:512:4], TOP, None, A.mult, deps=(s_kt,), cross=True)
     b_e0 = op("g", "bc", (T.e0b2[:], T.e0r2[0:1, :], 128), (x_e0r,))
-    x_w = v("quant", T.wq[:], T.ws[:], T.wt[:], deps=(ld_w,), cross=True)
+    v("tt", T.key2[:], T.kt[:], T.eidx[:], A.add, deps=())
 
     sc_done = []
     order = [(me, x_h0)] + [((me - q) % N, sem) for sem, qs, n in TIERS for q in qs]
@@ -257,17 +250,22 @@ def rank_program(g, core, T, topo):
     v("tr", T.gt[:], T.ps[:, 0:128], deps=(m,))
     x_sp = v("tt", T.sp[:, 4 * me:4 * me + 4], T.gt[:, 0:128:32], T.bt[:, 0:128:32], A.add, cross=True)
     send("ae", lambda q: T.sp[:, 4 * me:4 * me + 4], lambda d: T.sp[:, 4 * me:4 * me + 4], (x_sp,))
+    x_w = v("quant", T.wq[:], T.ws[:], T.wt[:], deps=(ld_w,), cross=True)
+    v("set", T.d1[:], 0.0, deps=())
+    v("set", T.rst[:, 128:512], 0.0, deps=())
     e0table(T.e0b2[:], ("v", b_e0))
+    v("set", T.rst[:, 128:512:4], -1.0e29)
 
-    v("copy", T.d1[:, 0:512:32], T.sp[:, 0:16], deps=("ae", x_sp))
+    v("copy", T.d1[:, 0:512:32], T.sp[:, 0:16], deps=("v", "ae", x_sp))
     s_rp = op("s", "act", (T.rp[:, 512:1024], T.sp[:].indirect(T.repo[:]), CP), ("ae", x_sp, x_rep))
     v("scan", T.rp[:, 0:512], T.hold32[:], T.d1[:], 0.0, A.mult, A.add)
     v("tr", T.sc2[:, 0:512], T.rp[:, 0:512])
     x_s2 = v("tr", T.sc2[:, 512:1024], T.rp[:, 512:1024], deps=(s_rp,), cross=True)
 
+    wait("v", ("v", x_s2))
+    x_s3 = v("copy", T.gv[:, 0:256], T.sc2[:].indirect(T.off2[:, 0:16]), deps=())
     s_g2 = op("s", "act", (T.gv[:, 256:512], T.sc2[:].indirect(T.off2[:, 16:32]), CP), (x_s2,))
-    v("copy", T.gv[:, 0:256], T.sc2[:].indirect(T.off2[:, 0:16]), deps=("v", x_s2))
-    wait("v", ("v", s_g2))
+    wait("v", (x_s3, s_g2))
     x_st2 = choose(512, T.key2)
     x_z2 = v("ts", T.zi2[:], T.st[:, 3:512:4], TOP, None, A.mult, deps=(x_st2,), cross=True)
     b_z = op("g", "bc", (T.zb2[:], T.zi2[0:1, :], 128), (x_z2,))

@@ -24,9 +24,10 @@ SCRATCH = {
     "mask16": _sb(128, B), "ci": _sb(128, I), "repo": _sb(32, U16), "rsh": _sb(32, I), "dupo": _sb(16, U16),
     "io1": _sb(1024, F), "eidx": _sb(512, F),
     "off1": _sb(32, U16), "offq": _sb(8, U16), "off2": _sb(32, U16), "er": _sb(512, F), "kt": _sb(512, F),
-    "key1": _sb(128, F), "key2": _sb(512, F), "e0r2": _sb(128, F), "e0b2": _sb(128, F), "ew": _sb(128, F), "es": _sb(128, F),
+    "eq": _sb(128, F), "flg": _sb(128, B), "key2": _sb(512, F), "e0r2": _sb(128, F), "e0b2": _sb(128, F), "ew": _sb(128, F),
+    "es": _sb(128, F),
     "sc": _sb(1024, F), "gv": _sb(512, F), "mx": _sb(512, F), "pm": _sb(512, B), "st": _sb(512, F),
-    "zrow": _sb(128, F), "zi1": _sb(128, I), "zi2": _sb(128, I), "zb2": _sb(128, I),
+    "mkr": _sb(128, B), "ct": _sb(8, F), "zi2": _sb(128, I), "zb2": _sb(128, I),
     "sj": _sb(128, I), "cj": _sb(128, I), "mk": _sb(128, B), "cw": _sb(128, F), "cum": _sb(128, B), "cs": _sb(128, F),
     "vv": _sb(128, B), "v2": _sb(256, B), "vt": _sb(256, B), "vs": _sb(256, B), "ov": _sb(8, F), "df": _sb(8, F), "od": _sb(8, F),
     "cf": _sb(8, F), "cu1": _sb(8, U16), "cu2": _sb(8, U16),
@@ -42,9 +43,9 @@ SCRATCH = {
 }
 
 REMOTE = ["al", "a0a", "a0b", "a0c", "ae", "a2", "left"]
-SEMAPHORES = REMOTE + ["v"] + ["s%d" % i for i in range(130)]
+SEMAPHORES = REMOTE + ["v"] + ["s%d" % i for i in range(140)]
 A = AluOpType
-CP = ActivationFunctionType.Copy
+CP, IDN = ActivationFunctionType.Copy, ActivationFunctionType.Identity
 TOP = 2.0 ** 19
 TIERS = (("a0a", (1, 2, 3, 4), 2), ("a0b", (5, 6), 4), ("a0c", (7,), 8))
 
@@ -111,20 +112,29 @@ def rank_program(g, core, T, topo):
     ld_e0 = dma("y", T.e0t[:], T.e0[:])
     ld_ps = dma("s", T.pst[:], T.p2[:])
     ld_u = dma("s", T.ut[:], T.u[:, 0:4])
+    ld_own = dma("s", T.pl[0], T.p2[:])
     ld_l1 = None
     for k in range(8):
-        ld_l1 = dma("s", T.l1[16 * k:16 * k + 16, :], T.p1[:], (), ld_l1)
-    ld_own = dma("s", T.pl[0], T.p2[:])
+        ld_l1 = dma("y", T.l1[16 * k:16 * k + 16, :], T.p1[:], (), ld_l1)
     ld_a = dma("y", T.at[:], T.a[:])
+    ld_l2 = dma("y", T.l2[:], T.pl[:], ("al", ld_own))
+    wait("y", [sem for sem, qs, n in TIERS])
     ld_e1 = dma("y", T.e1t[:], T.e1[:])
     ld_w = dma("y", T.wt[:], T.w[:])
     ld_e2 = dma("y", T.e2t[:], T.e2[:])
 
     i_p = op("g", "iota", (T.pidx[:], [[0, 1]], 0, 1))
-    i_1 = op("g", "iota", (T.io1[:], [[1, 1024]], 0, 0), allow_small_or_imprecise_dtypes=True)
+    i_0 = op("g", "iota", (T.io1[:, 0:128], [[1, 128]], 0, 0), allow_small_or_imprecise_dtypes=True)
+    i_1 = fresh()
+    for k in range(1, 8):
+        op("s", "act", (T.io1[:, 128 * k:128 * k + 128], T.io1[:, 0:128], IDN), (i_0,), sem=i_1, bias=float(128 * k))
     v("set", T.ones[:], 1.0)
     v("ts", T.r15[:], T.pidx[:], 15, None, A.bitwise_and, deps=(i_p,))
     v("ts", T.r31[:], T.pidx[:], 31, None, A.bitwise_and, deps=())
+    v("copy", T.ci[:], T.io1[:, 0:128], deps=(i_0,))
+    for buf, c in ((T.hold32[:, 0:256], 1.0), (T.hold16[:], 1.0), (T.rst[:, 0:128], 0.0), (T.pm[:, 0:512:4], 1.0), (T.ce[:, 0:128:4], 0.0),
+                   (T.mb[:, 0:1], 0.0)):
+        v("set", buf, c, deps=())
 
     send("al", lambda q: T.pst[:], lambda d: T.pl[(me - d) % N], (ld_ps,))
     x_h0 = v("quant", T.hall[:, mine], T.halls[:, mine], T.e0t[:], deps=(ld_e0,), cross=True)
@@ -132,7 +142,6 @@ def rank_program(g, core, T, topo):
         send(sem, lambda q: T.hall[:, mine].bitcast(dt.uint8), lambda d: T.hall[:, mine].bitcast(dt.uint8), (x_h0,), qs, n)
         send(sem, lambda q: T.halls[:, mine], lambda d: T.halls[:, mine], (x_h0,), qs, n)
 
-    ld_l2 = dma("y", T.l2[:], T.pl[:], ("al", ld_own))
     s_e = op("s", "act", (T.eidx[:], T.io1[:, 0:512], CP), (i_1,), scale=1024.0 / TOP)
 
     for a in range(4):
@@ -141,24 +150,23 @@ def rank_program(g, core, T, topo):
     for t in range(4):
         v("ts", T.ubig[:, t:512:4], T.ones[:], T.ut[:, t:t + 1], None, A.mult, deps=("v", ld_u) if t == 0 else ())
     x_off1 = v("copy", T.ip[:], T.r15[:], cross=True)
-    s_gq = op("s", "act", (T.gv[:, 0:128], T.io1[:].indirect(T.offq[:]), CP), (x_off1, i_1), scale=1.0 / TOP)
+    s_gq = op("s", "act", (T.eq[:], T.io1[:].indirect(T.offq[:]), CP), (x_off1, i_0))
     s_er = op("s", "act", (T.er[:], T.io1[:].indirect(T.off1[:]), CP))
-    for buf, c in ((T.hold32[:], 1.0), (T.hold16[:], 1.0), (T.rst[:, 0:128], 0.0), (T.pm[:, 0:512:4], 1.0), (T.mb[:, 0:1], 0.0)):
-        v("set", buf, c, deps=())
-    v("copy", T.ci[:], T.io1[:, 0:128], deps=(i_1,))
     x_u = v("quant", T.uq[:], T.us[:], T.ubig[:], deps=("v",), cross=True)
-    v("set", T.hold32[:, 0:512:32], 0.0, deps=())
+    v("set", T.hold32[:, 0:256:32], 0.0, deps=())
     v("set", T.hold16[:, 0:128:16], 0.0, deps=())
     v("set", T.rst[:, 0:128:4], -1.0e29, deps=())
     v("copy", T.sp31[:], T.r31[:], deps=())
     v("ts", T.cmod[:], T.ci[:], 15, None, A.bitwise_and, deps=())
     v("ts", T.rsh[:], T.ci[:, 0:32], 1, None, A.logical_shift_right, deps=())
+    v("copy", T.cj[:], T.eq[:], deps=(s_gq,))
     v("ts", T.spx[:], T.sp31[:], float(me), 99.0, A.is_equal, A.mult, deps=("v", x_off1))
+    v("ts", T.sj[:], T.cj[:], 7, None, A.logical_shift_right, deps=())
     v("ts", T.mask16[:], T.cmod[:], T.ip[:], None, A.is_equal, deps=())
     v("ts", T.dupo[:], T.rsh[:, 0:16], 16.0, T.ip[:], A.mult, A.add, deps=())
     x_rep = v("ts", T.repo[:], T.rsh[:], 16.0, None, A.add, deps=(), cross=True)
     v("tt", T.spart[:], T.spx[:], T.sp31[:], A.add)
-    v("tt", T.key1[:], T.gv[:, 0:128], T.eidx[:, 0:128], A.add, deps=(s_gq, s_e))
+    v("ts", T.flg[:], T.sj[:], T.spart[:], None, A.is_equal)
 
     def e0table(row, deps):
         v("tt", T.ew[:], row, T.mask16[:], A.mult, deps=deps)
@@ -168,9 +176,6 @@ def rank_program(g, core, T, topo):
     x_a = v("quant", T.aq[:], T.asc[:], T.at[:], deps=(ld_a,), cross=True)
     x_off2 = v("copy", T.off2[:], T.l2[:], deps=(ld_l2,), cross=True)
     s_kt = op("s", "act", (T.kt[:], T.io1[:].indirect(T.off2[:]), CP), (x_off2,), scale=1.0 / TOP)
-    x_e0r = v("ts", T.e0r2[:], T.kt[:, 0:512:4], TOP, None, A.mult, deps=(s_kt,), cross=True)
-    b_e0 = op("g", "bc", (T.e0b2[:], T.e0r2[0:1, :], 128), (x_e0r,))
-    v("tt", T.key2[:], T.kt[:], T.eidx[:], A.add, deps=())
 
     sc_done = []
     order = [(me, x_h0)] + [((me - q) % N, sem) for sem, qs, n in TIERS for q in qs]
@@ -184,37 +189,35 @@ def rank_program(g, core, T, topo):
             sc_done.append(op("s", "act", (T.sc[:, cs], bank, CP), (m,)))
     arrived = [x_h0] + [sem for sem, qs, n in TIERS]
 
-    def choose(w, key):
+    def marks(w):
         v("scan", T.mx[:, 0:w], T.rst[:, 0:w], T.gv[:, 0:w], 0.0, A.add, A.max)
         for k in (1, 2, 3):
             v("tt", T.pm[:, k:w:4], T.gv[:, k:w:4], T.mx[:, k - 1:w:4], A.is_gt, deps=("v",) if k == 1 else ())
-        return v("scan", T.st[:, 0:w], T.pm[:, 0:w], key[:], 0.0, A.max, A.min, cross=True)
 
-    def quarters(out, src, x):
+    def quarters(out, src, x, half=2):
         sem = fresh()
         for b in range(4):
             for a in range(4):
-                if b < 2:
+                if b < half:
                     v("copy", out(a, b), src(a), deps=(x,))
                 else:
                     op("s", "act", (out(a, b), src(a), CP), (x,), sem=sem)
         return sem
 
-    def capacity(zi, deps):
-        v("ts", T.sj[:], zi, 7, 7, A.logical_shift_right, A.bitwise_and, deps=deps)
-        v("ts", T.cj[:], zi, 1023, None, A.bitwise_and, deps=())
-        v("ts", T.mk[:], T.sj[:], T.spart[:], None, A.is_equal)
-        v("scan", T.cum[:], T.ones[:], T.mk[:], 0.0, A.mult, A.add)
-        v("tt", T.cw[:], T.cj[:], T.mask16[:], A.mult, deps=())
-        v("tt", T.vv[:], T.mk[:], T.cum[:], A.mult)
-        v("scan", T.cs[:], T.hold16[:], T.cw[:], 0.0, A.mult, A.add, deps=())
+    def capacity(mk, ctab, deps, mid=None):
+        v("scan", T.cum[:], T.ones[:], mk, 0.0, A.mult, A.add, deps=deps)
+        if mid:
+            mid()
+        v("tt", T.vv[:], mk, T.cum[:], A.mult)
+        if mid:
+            v("scan", T.cs[:], T.hold16[:], T.cw[:], 0.0, A.mult, A.add, deps=())
         v("copy", T.v2[:], T.vv[:].indirect(T.dupo[:]))
         v("tr", T.vt[:], T.v2[:])
-        v("tt", T.df[:], T.es[:, 15:128:16], T.cs[:, 15:128:16], A.subtract, deps=())
+        v("tt", T.df[:], T.es[:, 15:128:16], ctab[0], A.subtract, deps=ctab[1])
         v("scan", T.vs[:], T.hold32[:, 0:256], T.vt[:], 0.0, A.mult, A.add)
         v("ts", T.ov[:], T.vs[:, 31:256:32], 16.5, None, A.is_gt)
         v("tt", T.od[:], T.ov[:], T.df[:], A.mult)
-        v("tt", T.cf[:], T.od[:], T.cs[:, 15:128:16], A.add)
+        v("tt", T.cf[:], T.od[:], ctab[0], A.add)
 
     def update(hs, h, X, Xs, e, ld_e, deps, between):
         dep = []
@@ -227,22 +230,30 @@ def rank_program(g, core, T, topo):
             v("tt", h[:, i:512:4], hs[:, 128 * i:128 * i + 128], e[:, i:512:4], A.add, deps=(dep[i], ld_e))
 
     v("copy", T.gv[:, 0:128], T.sc[:].indirect(T.offq[:]), deps=["v"] + sc_done)
-    x_st = choose(128, T.key1)
-    s_z = quarters(lambda a, b: T.zrow[32 * b:32 * b + 32, 32 * a:32 * a + 32], lambda a: T.st[32 * a:32 * a + 32, 3:128:4], x_st)
-    v("ts", T.zi1[:], T.zrow[:], TOP, None, A.mult, deps=("v", s_z))
-    capacity(T.zi1[:], ("v",))
+    marks(128)
+    for k in (1, 2, 3):
+        v("tt", T.ce[:, k:128:4], T.gv[:, k:128:4], T.mx[:, k - 1:128:4], A.is_le, deps=())
+    v("tt", T.vv[:], T.pm[:, 0:128], T.flg[:], A.mult)
+    v("tt", T.ew[:], T.pm[:, 0:128], T.eq[:], A.mult, deps=())
+    x_pp = v("scan", T.pp[:], T.ce[:], T.vv[:], 0.0, A.mult, A.add, cross=True)
+    v("scan", T.ks[:], T.ce[:], T.ew[:], 0.0, A.mult, A.add, deps=())
+    s_mk = quarters(lambda a, b: T.mkr[32 * b:32 * b + 32, 32 * a:32 * a + 32], lambda a: T.pp[32 * a:32 * a + 32, 3:128:4], x_pp)
+    v("tt", T.lr[:], T.ks[:, 3:128:4], T.mask16[:, 0:32], A.mult)
+    x_lt = v("scan", T.lt[:], T.hold16[:, 0:32], T.lr[:], 0.0, A.mult, A.add, cross=True)
+    s_ct = quarters(lambda a, b: T.ct[32 * b:32 * b + 32, 2 * a:2 * a + 2], lambda a: T.lt[32 * a:32 * a + 32, 15:32:16], x_lt, 0)
+    capacity(T.mkr[:], (T.ct[:], (s_ct,)), ("v", s_mk))
     x_c1 = v("copy", T.cu1[:], T.cf[:], cross=True)
     s_x1 = op("s", "act", (T.x1s[:], T.halls[:].indirect(T.cu1[:]), CP), [x_c1] + arrived)
     x_x1 = v("copy", T.x1[:].bitcast(dt.uint32), T.hall[:].bitcast(dt.uint32).indirect(T.cu1[:]), deps=[x_c1] + arrived, cross=True)
-    cross1 = []
+    rows = []
 
     def between1():
         v("copy", T.base1[:], T.sc[:].indirect(T.cu1[:]), deps=("v", x_c1))
-        cross1.append(v("copy", T.chr1[:], T.io1[:].indirect(T.cu1[:]), deps=(), cross=True))
+        rows.append(v("copy", T.chr1[:], T.io1[:].indirect(T.cu1[:]), deps=(), cross=True))
         v("tr", T.bt[:], T.base1[:])
 
     update(T.hs1, T.h1, T.x1, T.x1s, T.e1t, ld_e1, (x_x1, s_x1, x_a), between1)
-    dma("y", T.ch[0:1, :], T.chr1[0:1, :], (cross1[0],))
+    dma("y", T.ch[0:1, :], T.chr1[0:1, :], (rows[0],))
     x_h1 = v("quant", T.h1q[:], T.h1s[:], T.h1[:], cross=True)
 
     m = op("t", "mm", (T.ps[:, 0:128], T.uq[:], T.us[:], T.h1q[:], T.h1s[:], True, True), (x_h1,))
@@ -250,11 +261,17 @@ def rank_program(g, core, T, topo):
     v("tr", T.gt[:], T.ps[:, 0:128], deps=(m,))
     x_sp = v("tt", T.sp[:, 4 * me:4 * me + 4], T.gt[:, 0:128:32], T.bt[:, 0:128:32], A.add, cross=True)
     send("ae", lambda q: T.sp[:, 4 * me:4 * me + 4], lambda d: T.sp[:, 4 * me:4 * me + 4], (x_sp,))
-    x_w = v("quant", T.wq[:], T.ws[:], T.wt[:], deps=(ld_w,), cross=True)
+
+    x_e0r = v("ts", T.e0r2[:], T.kt[:, 0:512:4], TOP, None, A.mult, deps=(s_kt,), cross=True)
+    b_e0 = op("g", "bc", (T.e0b2[:], T.e0r2[0:1, :], 128), (x_e0r,))
     v("set", T.d1[:], 0.0, deps=())
+    v("set", T.hold32[:, 256:512], 1.0, deps=())
     v("set", T.rst[:, 128:512], 0.0, deps=())
+    v("tt", T.key2[:], T.kt[:], T.eidx[:], A.add, deps=(s_e,))
+    x_w = v("quant", T.wq[:], T.ws[:], T.wt[:], deps=(ld_w,), cross=True)
     e0table(T.e0b2[:], ("v", b_e0))
-    v("set", T.rst[:, 128:512:4], -1.0e29)
+    v("set", T.hold32[:, 256:512:32], 0.0)
+    v("set", T.rst[:, 128:512:4], -1.0e29, deps=())
 
     v("copy", T.d1[:, 0:512:32], T.sp[:, 0:16], deps=("v", "ae", x_sp))
     s_rp = op("s", "act", (T.rp[:, 512:1024], T.sp[:].indirect(T.repo[:]), CP), ("ae", x_sp, x_rep))
@@ -266,8 +283,9 @@ def rank_program(g, core, T, topo):
     x_s3 = v("copy", T.gv[:, 0:256], T.sc2[:].indirect(T.off2[:, 0:16]), deps=())
     s_g2 = op("s", "act", (T.gv[:, 256:512], T.sc2[:].indirect(T.off2[:, 16:32]), CP), (x_s2,))
     wait("v", (x_s3, s_g2))
-    x_st2 = choose(512, T.key2)
-    x_z2 = v("ts", T.zi2[:], T.st[:, 3:512:4], TOP, None, A.mult, deps=(x_st2,), cross=True)
+    marks(512)
+    v("scan", T.st[:], T.pm[:], T.key2[:], 0.0, A.max, A.min)
+    x_z2 = v("ts", T.zi2[:], T.st[:, 3:512:4], TOP, None, A.mult, cross=True)
     b_z = op("g", "bc", (T.zb2[:], T.zi2[0:1, :], 128), (x_z2,))
     v("ts", T.am[:], T.zi2[:], 896, None, A.bitwise_and, deps=(x_z2,))
     v("ts", T.mb[:, 1:129], T.am[:], float(128 * me), None, A.is_equal)
@@ -287,9 +305,12 @@ def rank_program(g, core, T, topo):
     send("a2", lambda q: T.pk[:, 16 * q:16 * q + 16].bitcast(dt.uint8), lambda d: T.win2[:, land].bitcast(dt.uint8), (x_pk,))
     send("a2", lambda q: T.pks[:, 16 * q:16 * q + 16], lambda d: T.win2s[:, land], (s_pk,))
 
-    capacity(T.zb2[:], (b_z,))
-    x_c2 = v("copy", T.cu2[:], T.cf[:], cross=True)
+    v("ts", T.sj[:], T.zb2[:], 7, 7, A.logical_shift_right, A.bitwise_and, deps=(b_z,))
+    v("ts", T.cj[:], T.zb2[:], 1023, None, A.bitwise_and, deps=())
+    v("ts", T.mk[:], T.sj[:], T.spart[:], None, A.is_equal)
     cnt, ctab = T.vs[:, 31:256:32], T.cs[:, 15:128:16]
+    capacity(T.mk[:], (ctab, ()), ("v",), lambda: v("tt", T.cw[:], T.cj[:], T.mask16[:], A.mult, deps=()))
+    x_c2 = v("copy", T.cu2[:], T.cf[:], cross=True)
     v("copy", T.ti[:], ctab, deps=())
     v("ts", T.isr[:], cnt, 0.5, None, A.is_gt, deps=())
     v("ts", T.own[:], T.cf[:], float(128 - 128 * me), None, A.add, deps=())
@@ -301,21 +322,24 @@ def rank_program(g, core, T, topo):
     v("tt", T.de[:], T.dd[:], T.isk[:], A.mult)
     v("tt", T.ix[:], T.de[:], T.own[:], A.add)
     x_ix = v("copy", T.ixu[:], T.ix[:], cross=True)
-    v("copy", T.base2[:], T.sc2[:].indirect(T.cu2[:]), deps=("v", x_c2))
-    x_ch2 = v("copy", T.chr2[:], T.io1[:].indirect(T.cu2[:]), deps=(), cross=True)
-    dma("y", T.ch[1:2, :], T.chr2[0:1, :], (x_ch2,))
     s_x2 = op("s", "act", (T.x2s[:], T.win2s[:].indirect(T.ixu[:]), CP), (x_ix, "a2"))
     x_x2 = v("copy", T.x2[:].bitcast(dt.uint32), T.win2[:].bitcast(dt.uint32).indirect(T.ixu[:]), deps=(x_ix, "a2"), cross=True)
-    update(T.hs2, T.h2, T.x2, T.x2s, T.e2t, ld_e2, (x_x2, s_x2, x_a), lambda: None)
+
+    def between2():
+        v("copy", T.base2[:], T.sc2[:].indirect(T.cu2[:]), deps=("v", x_c2))
+        rows.append(v("copy", T.chr2[:], T.io1[:].indirect(T.cu2[:]), deps=(), cross=True))
+
+    update(T.hs2, T.h2, T.x2, T.x2s, T.e2t, ld_e2, (x_x2, s_x2, x_a), between2)
+    dma("y", T.ch[1:2, :], T.chr2[0:1, :], (rows[1],))
     x_h2 = v("quant", T.h2q[:], T.h2s[:], T.h2[:], cross=True)
 
     m_y = op("t", "mm", (T.ps[:, 512:640], T.wq[:], T.ws[:], T.h2q[:], T.h2s[:], True, True), (x_h2, x_w))
     m_g = op("t", "mm", (T.ps[:, 0:128], T.uq[:], T.us[:], T.h2q[:], T.h2s[:], True, True), (x_h2,))
-    s_y = op("s", "act", (T.yt[:], T.ps[:, 512:640], CP), (m_y,))
-    x_g = v("tt", T.gout[:], T.ps[:, 0:128], T.base2[:], A.add, deps=("v", m_g), cross=True)
     dma("y", T.oc[:], T.h2q[:].bitcast(dt.uint8), (x_h2,))
     for k in range(4):
-        dma("y", T.osc[4 * k:4 * k + 4, :], T.h2s[32 * k:32 * k + 4, :], (x_h2,))
+        dma("ys"[k // 2], T.osc[4 * k:4 * k + 4, :], T.h2s[32 * k:32 * k + 4, :], (x_h2,))
+    s_y = op("s", "act", (T.yt[:], T.ps[:, 512:640], CP), (m_y,))
+    x_g = v("tt", T.gout[:], T.ps[:, 0:128], T.base2[:], A.add, deps=("v", m_g), cross=True)
     dma("s", T.y[:], T.yt[:], (s_y,))
     dma("y", T["g"][:], T.gout[0:1, :], (x_g,))
 

@@ -13,7 +13,7 @@ SCRATCH = {
     "e0t": _sb(512, B), "e1t": _sb(512, B), "e2t": _sb(512, B), "at": _sb(2048, B), "wt": _sb(512, B), "ut": _sb(4, B),
     "ubig": _sb(512, B),
     "pst": ("dram", [128, 4], I), "pl": ("dram", [8, 128, 4], I),
-    "l1": _sb(32, I), "l2": _sb(32, I),
+    "l1": _sb(32, I), "lo": _sb(32, I), "l2": _sb(32, I),
     "uq": _sb(128, X4), "us": _sb(128, U8), "aq": _sb(512, X4), "asc": _sb(512, U8), "wq": _sb(128, X4), "ws": _sb(128, U8),
     "hall": _sb(1024, X4), "halls": _sb(1024, U8), "x1": _sb(128, X4), "x1s": _sb(128, U8),
     "h1q": _sb(128, X4), "h1s": _sb(128, U8), "pk": _sb(128, X4), "pks": _sb(128, U8),
@@ -23,40 +23,93 @@ SCRATCH = {
     "r31": _sb(1, I), "ip": _sb(1, F), "sp31": _sb(1, F), "spx": _sb(1, F), "spart": _sb(1, F), "cmod": _sb(128, I),
     "mask16": _sb(128, B), "ci": _sb(128, I), "repo": _sb(32, U16), "rsh": _sb(32, I), "dupo": _sb(16, U16),
     "io1": _sb(1024, F), "eidx": _sb(512, F),
-    "off1": _sb(32, U16), "offq": _sb(8, U16), "off2": _sb(32, U16), "er": _sb(512, F), "kt": _sb(512, F),
-    "eq": _sb(128, F), "flg": _sb(128, B), "key2": _sb(512, F), "e0r2": _sb(128, F), "e0b2": _sb(128, F), "ew": _sb(128, F),
-    "es": _sb(128, F),
+    "off1": _sb(32, U16), "offo": _sb(32, U16), "offh": _sb(16, U16), "off2": _sb(32, U16), "er": _sb(512, F), "er2": _sb(512, F),
+    "kt": _sb(512, F), "kp": _sb(256, F), "key1": _sb(256, F), "key2": _sb(512, F), "st1": _sb(256, F),
+    "ew": _sb(128, F), "es": _sb(128, F), "ew2": _sb(128, F), "es2": _sb(128, F),
     "sc": _sb(1024, F), "gv": _sb(512, F), "mx": _sb(512, F), "pm": _sb(512, B), "st": _sb(512, F),
-    "mkr": _sb(128, B), "ct": _sb(8, F), "zi2": _sb(128, I), "zb2": _sb(128, I),
-    "sj": _sb(128, I), "cj": _sb(128, I), "mk": _sb(128, B), "cw": _sb(128, F), "cum": _sb(128, B), "cs": _sb(128, F),
-    "vv": _sb(128, B), "v2": _sb(256, B), "vt": _sb(256, B), "vs": _sb(256, B), "ov": _sb(8, F), "df": _sb(8, F), "od": _sb(8, F),
-    "cf": _sb(8, F), "cu1": _sb(8, U16), "cu2": _sb(8, U16),
+    "zb1": _sb(128, I), "zf1": _sb(128, F), "zi2": _sb(128, I), "zb2": _sb(128, I), "zrow": _sb(128, F), "zf2": _sb(128, F),
+    "sj": _sb(128, I), "mk": _sb(128, B), "th": _sb(128, B), "cum": _sb(128, B), "cs": _sb(128, F),
+    "dup1": _sb(256, B), "dup2": _sb(256, B), "v2": _sb(256, B), "vt": _sb(256, B), "vs": _sb(256, B),
+    "f8": _sb(160, F), "i8": _sb(32, I), "cu1": _sb(8, U16), "cu2": _sb(8, U16),
     "base1": _sb(128, F), "bt": _sb(128, F), "gt": _sb(128, F), "sp": _sb(32, F), "d1": _sb(512, F), "rp": _sb(1024, F),
     "sc2": _sb(1024, F), "base2": _sb(128, F), "gout": _sb(128, F), "yt": _sb(128, F),
     "am": _sb(128, I), "mb": _sb(144, B), "ce": _sb(128, B), "pp": _sb(128, B), "ks": _sb(128, F), "lr": _sb(32, F),
     "lt": _sb(32, F), "ls": _sb(32, F), "r8": _sb(8, F), "r8i": _sb(8, I), "r8n": _sb(8, I), "offp": _sb(8, U16),
-    "ti": _sb(8, I), "tsh": _sb(8, I), "t1": _sb(8, F), "t2": _sb(8, F), "isr": _sb(8, F), "isk": _sb(8, F), "own": _sb(8, F),
-    "dd": _sb(8, F), "de": _sb(8, F), "ix": _sb(8, F), "ixu": _sb(8, U16),
-    "chr1": _sb(128, F), "chr2": _sb(128, F),
+    "ixu": _sb(8, U16), "chr1": _sb(128, F), "chr2": _sb(128, F),
     "hs1": _sb(512, F), "hs2": _sb(512, F), "h1": _sb(512, B), "h2": _sb(512, B),
     "ps": ("psum", [128, 2048], F), "pr": ("psum", [128, 2048], F),
 }
 
-REMOTE = ["al", "a0a", "a0b", "a0c", "ae", "a2", "left"]
-SEMAPHORES = REMOTE + ["v"] + ["s%d" % i for i in range(140)]
+REMOTE = ["al", "a0a", "a0b", "a0c", "ae", "a2", "left", "hl", "kc", "ks"]
+SEMAPHORES = REMOTE + ["v"] + ["s%d" % i for i in range(135)]
 A = AluOpType
 CP, IDN = ActivationFunctionType.Copy, ActivationFunctionType.Identity
 TOP = 2.0 ** 19
-TIERS = (("a0a", (1, 2, 3, 4), 2), ("a0b", (5, 6), 4), ("a0c", (7,), 8))
+
+TIERS = (("a0a", {1: 2, 2: 2, 3: 2, 4: 2}), ("a0b", {5: 4, 6: 4}), ("a0c", {7: 8}))
+LISTS = ({1: 2, 2: 2, 3: 2, 4: 2}, {5: 2, 6: 2, 7: 4})
+SCORES = {q: 1 for q in range(1, 8)}
+PICKS, PICKS_H = {1: 2, 2: 2, 3: 4}, ({4: 4, 5: 4}, {6: 4, 7: 4})
+
+
+def helpers(core, topo):
+    return [c for c in topo.cores_of(core) if topo.die(c) != topo.die(core)][:len(LISTS)]
+
+
+def fused(g, T, topo, core, parts):
+    tr = []
+    for c, e, sem, src, dst in parts:
+        rid, pid = topo.addr(c, core)
+        tr.append(RemoteDMATransfer(dst_ids=[DstId(rid=rid, pnc=pid)], dma_engine_mask=sum(1 << x for x in e), remote_sem=T.sem[sem],
+                                    srcs=[src], dsts=[dst]))
+    g.remote_dma_fused(tr, local_sem=T.sem.left)
+    return sum(len(e) for c, e, sem, src, dst in parts)
+
+
+def far(T, topo, core, me, share, sem, src, dst):
+    parts, at = [], 0
+    for q, n in share.items():
+        d = (me + q) % len(T.cores)
+        parts.append((T.cores[d], topo.engines(core, T.cores[d])[at:at + n], sem, src(q), dst(d)))
+        at += n
+    return parts
+
+
+def near(T, topo, core, me, sem, src):
+    hp = helpers(core, topo)
+    away = topo.engines(core, T.cores[(me + 1) % len(T.cores)])
+    e = [x for x in topo.engines(core, hp[0]) if x not in away]
+    n = len(e) // len(hp)
+    return [(c, e[n * i:n * i + n], sem, src(i), src(i)) for i, c in enumerate(hp)]
+
+
+def pick_calls(T, me):
+    land = slice(16 * me, 16 * me + 16)
+    return (("kc", lambda q: T.pk[:, 16 * q:16 * q + 16].bitcast(dt.uint8), lambda d: T.win2[:, land].bitcast(dt.uint8)),
+            ("ks", lambda q: T.pks[:, 16 * q:16 * q + 16], lambda d: T.win2s[:, land]))
+
+
+def helper_program(g, core, T, topo, me, k):
+    N = len(T.cores)
+    n = len(near(T, topo, T.cores[me], me, "hl", lambda i: None)[k][1])
+    g.wait_ge(T.sem.hl, n)
+    left = fused(g, T, topo, core, far(T, topo, core, me, LISTS[k], "al", lambda q: T.pst[:], lambda d: T.pl[(me - d) % N]))
+    for sem, src, dst in pick_calls(T, me):
+        g.wait_ge(T.sem[sem], n)
+        left += fused(g, T, topo, core, far(T, topo, core, me, PICKS_H[k], "a2", src, dst))
+    g.wait_ge(T.sem.left, left)
 
 
 def rank_program(g, core, T, topo):
     me = T.rank_of(core)
     if me is None:
+        for r, c in enumerate(T.cores):
+            if core in helpers(c, topo):
+                helper_program(g, core, T, topo, r, helpers(c, topo).index(core))
         return
     N = len(T.cores)
     Q = {"g": g, "v": g.vector, "s": g.scalar, "t": g.tensor, "y": g.sync}
-    total, seen, used = {}, {}, [0]
+    total, seen, used = {"left": 0}, {}, [0]
 
     def wait(q, deps):
         for sem in deps:
@@ -91,35 +144,33 @@ def rank_program(g, core, T, topo):
     def v(name, *args, deps=("v",), cross=False):
         return op("v", name, args, deps, cross)
 
-    def send(sem, src, dst, deps, qs=range(1, N), n=1):
+    def send(parts, deps):
         wait("g", deps)
-        tr = []
-        for i, q in enumerate(qs):
-            d = (me + q) % N
-            c = T.cores[d]
-            rid, pid = topo.addr(c, core)
-            e = topo.engines(core, c)
-            tr.append(RemoteDMATransfer(dst_ids=[DstId(rid=rid, pnc=pid)], dma_engine_mask=sum(1 << x for x in e[i * n:i * n + n]),
-                                        remote_sem=T.sem[sem], srcs=[src(q)], dsts=[dst(d)]))
-        g.remote_dma_fused(tr, local_sem=T.sem.left)
-        total["left"] = total.get("left", 0) + n * len(tr)
+        total["left"] += fused(g, T, topo, core, parts)
 
-    total["al"], total["ae"], total["a2"] = N - 1, N - 1, 2 * (N - 1)
-    for sem, qs, n in TIERS:
-        total[sem] = 2 * n * len(qs)
+    def count(*shares):
+        return sum(n for share in shares for n in share.values())
+
+    total["al"], total["ae"], total["a2"] = count(*LISTS), count(SCORES), 2 * count(PICKS, *PICKS_H)
+    for sem, share in TIERS:
+        total[sem] = 2 * count(share)
+    arrivals = [sem for sem, share in TIERS]
     mine = slice(128 * me, 128 * me + 128)
 
     ld_e0 = dma("y", T.e0t[:], T.e0[:])
     ld_ps = dma("s", T.pst[:], T.p2[:])
     ld_u = dma("s", T.ut[:], T.u[:, 0:4])
     ld_own = dma("s", T.pl[0], T.p2[:])
-    ld_l1 = None
+    ld_l1, ld_lo = None, None
     for k in range(8):
         ld_l1 = dma("y", T.l1[16 * k:16 * k + 16, :], T.p1[:], (), ld_l1)
+    for k in range(8):
+        ld_lo = dma("y", T.lo[16 * k:16 * k + 16, :], T.p2[:], (), ld_lo)
+    wait("y", arrivals[:1])
     ld_a = dma("y", T.at[:], T.a[:])
-    ld_l2 = dma("y", T.l2[:], T.pl[:], ("al", ld_own))
-    wait("y", [sem for sem, qs, n in TIERS])
+    wait("y", arrivals)
     ld_e1 = dma("y", T.e1t[:], T.e1[:])
+    ld_l2 = dma("y", T.l2[:], T.pl[:], ("al", ld_own))
     ld_w = dma("y", T.wt[:], T.w[:])
     ld_e2 = dma("y", T.e2t[:], T.e2[:])
 
@@ -132,146 +183,142 @@ def rank_program(g, core, T, topo):
     v("ts", T.r15[:], T.pidx[:], 15, None, A.bitwise_and, deps=(i_p,))
     v("ts", T.r31[:], T.pidx[:], 31, None, A.bitwise_and, deps=())
     v("copy", T.ci[:], T.io1[:, 0:128], deps=(i_0,))
-    for buf, c in ((T.hold32[:, 0:256], 1.0), (T.hold16[:], 1.0), (T.rst[:, 0:128], 0.0), (T.pm[:, 0:512:4], 1.0), (T.ce[:, 0:128:4], 0.0),
-                   (T.mb[:, 0:1], 0.0)):
+    for buf, c in ((T.hold32[:, 0:256], 1.0), (T.hold16[:], 1.0), (T.rst[:, 0:256], 0.0), (T.pm[:, 0:512:4], 1.0), (T.mb[:, 0:1], 0.0)):
         v("set", buf, c, deps=())
 
-    send("al", lambda q: T.pst[:], lambda d: T.pl[(me - d) % N], (ld_ps,))
     x_h0 = v("quant", T.hall[:, mine], T.halls[:, mine], T.e0t[:], deps=(ld_e0,), cross=True)
-    for sem, qs, n in TIERS:
-        send(sem, lambda q: T.hall[:, mine].bitcast(dt.uint8), lambda d: T.hall[:, mine].bitcast(dt.uint8), (x_h0,), qs, n)
-        send(sem, lambda q: T.halls[:, mine], lambda d: T.halls[:, mine], (x_h0,), qs, n)
+    for sem, share in TIERS:
+        for piece in (T.hall[:, mine].bitcast(dt.uint8), T.halls[:, mine]):
+            send(far(T, topo, core, me, share, sem, lambda q: piece, lambda d: piece), (x_h0,))
+    send(near(T, topo, core, me, "hl", lambda i: T.pst[:]), (ld_ps,))
 
     s_e = op("s", "act", (T.eidx[:], T.io1[:, 0:512], CP), (i_1,), scale=1024.0 / TOP)
 
-    for a in range(4):
-        v("copy", T.offq[32 * a:32 * a + 32, :], T.l1[32 * a:32 * a + 32, 8 * a:8 * a + 8], deps=(ld_l1,))
+    for a in range(2):
+        v("copy", T.offh[64 * a:64 * a + 64, :], T.l1[64 * a:64 * a + 64, 16 * a:16 * a + 16], deps=(ld_l1,))
     v("copy", T.off1[:], T.l1[:], deps=())
     for t in range(4):
         v("ts", T.ubig[:, t:512:4], T.ones[:], T.ut[:, t:t + 1], None, A.mult, deps=("v", ld_u) if t == 0 else ())
     x_off1 = v("copy", T.ip[:], T.r15[:], cross=True)
-    s_gq = op("s", "act", (T.eq[:], T.io1[:].indirect(T.offq[:]), CP), (x_off1, i_0))
+    s_kp = op("s", "act", (T.kp[:], T.io1[:].indirect(T.offh[:]), CP), (x_off1, i_1), scale=1.0 / TOP)
     s_er = op("s", "act", (T.er[:], T.io1[:].indirect(T.off1[:]), CP))
     x_u = v("quant", T.uq[:], T.us[:], T.ubig[:], deps=("v",), cross=True)
     v("set", T.hold32[:, 0:256:32], 0.0, deps=())
     v("set", T.hold16[:, 0:128:16], 0.0, deps=())
-    v("set", T.rst[:, 0:128:4], -1.0e29, deps=())
+    v("set", T.rst[:, 0:256:4], -1.0e29, deps=())
     v("copy", T.sp31[:], T.r31[:], deps=())
     v("ts", T.cmod[:], T.ci[:], 15, None, A.bitwise_and, deps=())
     v("ts", T.rsh[:], T.ci[:, 0:32], 1, None, A.logical_shift_right, deps=())
-    v("copy", T.cj[:], T.eq[:], deps=(s_gq,))
     v("ts", T.spx[:], T.sp31[:], float(me), 99.0, A.is_equal, A.mult, deps=("v", x_off1))
-    v("ts", T.sj[:], T.cj[:], 7, None, A.logical_shift_right, deps=())
     v("ts", T.mask16[:], T.cmod[:], T.ip[:], None, A.is_equal, deps=())
     v("ts", T.dupo[:], T.rsh[:, 0:16], 16.0, T.ip[:], A.mult, A.add, deps=())
     x_rep = v("ts", T.repo[:], T.rsh[:], 16.0, None, A.add, deps=(), cross=True)
     v("tt", T.spart[:], T.spx[:], T.sp31[:], A.add)
-    v("ts", T.flg[:], T.sj[:], T.spart[:], None, A.is_equal)
+    for a in range(2):
+        h = slice(64 * a, 64 * a + 64)
+        v("tt", T.key1[h, :], T.kp[h, :], T.eidx[h, 256 * a:256 * a + 256], A.add, deps=(s_kp, s_e))
 
-    def e0table(row, deps):
-        v("tt", T.ew[:], row, T.mask16[:], A.mult, deps=deps)
-        v("scan", T.es[:], T.hold16[:], T.ew[:], 0.0, A.mult, A.add)
+    def e0table(ew, es, row, deps):
+        v("tt", ew[:], row[:, 0:512:4], T.mask16[:], A.mult, deps=deps)
+        v("scan", es[:], T.hold16[:], ew[:], 0.0, A.mult, A.add)
 
-    e0table(T.er[:, 0:512:4], ("v", s_er))
-    x_a = v("quant", T.aq[:], T.asc[:], T.at[:], deps=(ld_a,), cross=True)
-    x_off2 = v("copy", T.off2[:], T.l2[:], deps=(ld_l2,), cross=True)
-    s_kt = op("s", "act", (T.kt[:], T.io1[:].indirect(T.off2[:]), CP), (x_off2,), scale=1.0 / TOP)
+    x_offo = v("copy", T.offo[:], T.lo[:], deps=(ld_lo,), cross=True)
+    s_er2 = op("s", "act", (T.er2[:], T.io1[:].indirect(T.offo[:]), CP), (x_offo,))
+    e0table(T.ew, T.es, T.er, ("v", s_er))
+    v("set", T.d1[:], 0.0, deps=())
+    v("set", T.hold32[:, 256:512], 1.0, deps=())
+    v("set", T.rst[:, 256:512], 0.0, deps=())
+    v("set", T.hold32[:, 256:512:32], 0.0)
+    v("set", T.rst[:, 256:512:4], -1.0e29, deps=())
+    e0table(T.ew2, T.es2, T.er2, ("v", s_er2))
 
     sc_done = []
-    order = [(me, x_h0)] + [((me - q) % N, sem) for sem, qs, n in TIERS for q in qs]
+    order = [(me, x_h0)] + [((me - q) % N, sem) for sem, share in TIERS for q in share]
     for i, (r, sem) in enumerate(order):
         cs = slice(128 * r, 128 * r + 128)
         bank = (T.ps if i < 4 else T.pr)[:, 512 * (i % 4):512 * (i % 4) + 128]
         m = op("t", "mm", (bank, T.uq[:], T.us[:], T.hall[:, cs], T.halls[:, cs], True, True), (x_u, sem))
         if i % 2:
-            v("copy", T.sc[:, cs], bank, deps=(m,))
+            sc_done.append(v("copy", T.sc[:, cs], bank, deps=(m,), cross=True))
         else:
             sc_done.append(op("s", "act", (T.sc[:, cs], bank, CP), (m,)))
-    arrived = [x_h0] + [sem for sem, qs, n in TIERS]
+    arrived = [x_h0] + arrivals
 
     def marks(w):
         v("scan", T.mx[:, 0:w], T.rst[:, 0:w], T.gv[:, 0:w], 0.0, A.add, A.max)
         for k in (1, 2, 3):
             v("tt", T.pm[:, k:w:4], T.gv[:, k:w:4], T.mx[:, k - 1:w:4], A.is_gt, deps=("v",) if k == 1 else ())
 
-    def quarters(out, src, x, half=2):
-        sem = fresh()
-        for b in range(4):
-            for a in range(4):
-                if b < half:
-                    v("copy", out(a, b), src(a), deps=(x,))
-                else:
-                    op("s", "act", (out(a, b), src(a), CP), (x,), sem=sem)
-        return sem
+    def f8(i):
+        return T.f8[:, 8 * i:8 * i + 8]
 
-    def capacity(mk, ctab, deps, mid=None):
-        v("scan", T.cum[:], T.ones[:], mk, 0.0, A.mult, A.add, deps=deps)
-        if mid:
-            mid()
-        v("tt", T.vv[:], mk, T.cum[:], A.mult)
-        if mid:
-            v("scan", T.cs[:], T.hold16[:], T.cw[:], 0.0, A.mult, A.add, deps=())
-        v("copy", T.v2[:], T.vv[:].indirect(T.dupo[:]))
-        v("tr", T.vt[:], T.v2[:])
-        v("tt", T.df[:], T.es[:, 15:128:16], ctab[0], A.subtract, deps=ctab[1])
-        v("scan", T.vs[:], T.hold32[:, 0:256], T.vt[:], 0.0, A.mult, A.add)
-        v("ts", T.ov[:], T.vs[:, 31:256:32], 16.5, None, A.is_gt)
-        v("tt", T.od[:], T.ov[:], T.df[:], A.mult)
-        v("tt", T.cf[:], T.od[:], ctab[0], A.add)
+    def i8(i):
+        return T.i8[:, 8 * i:8 * i + 8]
 
-    def update(hs, h, X, Xs, e, ld_e, deps, between):
+    etab, etab2, cnt = T.es[:, 15:128:16], T.es2[:, 15:128:16], T.vs[:, 31:256:32]
+
+    def update(hs, h, X, Xs, e, ld_e, deps, x_a, between):
         dep = []
         for i in range(4):
             s = slice(128 * i, 128 * i + 128)
-            m = op("t", "mm", (T.pr[:, 512 * i:512 * i + 128], T.aq[:, s], T.asc[:, s], X[:], Xs[:], True, True), deps)
+            m = op("t", "mm", (T.pr[:, 512 * i:512 * i + 128], T.aq[:, s], T.asc[:, s], X[:], Xs[:], True, True), tuple(deps) + (x_a[i],))
             dep.append(op("s", "act", (hs[:, s], T.pr[:, 512 * i:512 * i + 128], CP), (m,), scale=0.05))
         between()
         for i in range(4):
             v("tt", h[:, i:512:4], hs[:, 128 * i:128 * i + 128], e[:, i:512:4], A.add, deps=(dep[i], ld_e))
 
-    v("copy", T.gv[:, 0:128], T.sc[:].indirect(T.offq[:]), deps=["v"] + sc_done)
-    marks(128)
-    for k in (1, 2, 3):
-        v("tt", T.ce[:, k:128:4], T.gv[:, k:128:4], T.mx[:, k - 1:128:4], A.is_le, deps=())
-    v("tt", T.vv[:], T.pm[:, 0:128], T.flg[:], A.mult)
-    v("tt", T.ew[:], T.pm[:, 0:128], T.eq[:], A.mult, deps=())
-    x_pp = v("scan", T.pp[:], T.ce[:], T.vv[:], 0.0, A.mult, A.add, cross=True)
-    v("scan", T.ks[:], T.ce[:], T.ew[:], 0.0, A.mult, A.add, deps=())
-    s_mk = quarters(lambda a, b: T.mkr[32 * b:32 * b + 32, 32 * a:32 * a + 32], lambda a: T.pp[32 * a:32 * a + 32, 3:128:4], x_pp)
-    v("tt", T.lr[:], T.ks[:, 3:128:4], T.mask16[:, 0:32], A.mult)
-    x_lt = v("scan", T.lt[:], T.hold16[:, 0:32], T.lr[:], 0.0, A.mult, A.add, cross=True)
-    s_ct = quarters(lambda a, b: T.ct[32 * b:32 * b + 32, 2 * a:2 * a + 2], lambda a: T.lt[32 * a:32 * a + 32, 15:32:16], x_lt, 0)
-    capacity(T.mkr[:], (T.ct[:], (s_ct,)), ("v", s_mk))
-    x_c1 = v("copy", T.cu1[:], T.cf[:], cross=True)
+    v("copy", T.gv[:, 0:128], T.sc[:].indirect(T.offh[:, 0:8]), deps=["v"] + sc_done)
+    s_g1 = op("s", "act", (T.gv[:, 128:256], T.sc[:].indirect(T.offh[:, 8:16]), CP), sc_done)
+    wait("v", ("v", s_g1))
+    marks(256)
+    x_st1 = v("scan", T.st1[:], T.pm[:, 0:256], T.key1[:], 0.0, A.max, A.min, cross=True)
+    s_zf = fresh()
+    for b in range(2):
+        for a in range(2):
+            here, there, to = slice(64 * a, 64 * a + 64), slice(64 * b, 64 * b + 64), slice(64 * a, 64 * a + 64)
+            v("ts", T.zb1[there, to], T.st1[here, 3:256:4], TOP, None, A.mult, deps=(x_st1,))
+            op("s", "act", (T.zf1[there, to], T.st1[here, 3:256:4], CP), (x_st1,), sem=s_zf)
+
+    v("ts", T.sj[:], T.zb1[:], 7, 7, A.logical_shift_right, A.bitwise_and)
+    x_th = v("ts", T.th[:], T.sj[:], T.spart[:], 1.0e6, A.not_equal, A.mult, cross=True)
+    s_th = op("s", "act", (T.dup1[:], T.th[:].indirect(T.dupo[:]), CP), (x_th,))
+    v("ts", T.mk[:], T.sj[:], T.spart[:], None, A.is_equal, deps=())
+    v("scan", T.cum[:], T.ones[:], T.mk[:], -16.5, A.mult, A.add)
+    v("scan", T.cs[:], T.mask16[:], T.zf1[:], 0.0, A.max, A.min, deps=(s_zf,))
+    v("ts", i8(0), T.cs[:, 15:128:16], TOP, None, A.mult)
+    v("ts", i8(1), i8(0), 1023, None, A.bitwise_and)
+    v("tt", T.v2[:], T.cum[:].indirect(T.dupo[:]), T.dup1[:], A.is_gt, deps=("v", s_th))
+    v("tt", f8(0), etab, i8(1), A.subtract, deps=())
+    v("tr", T.vt[:], T.v2[:])
+    v("scan", T.vs[:], T.hold32[:, 0:256], T.vt[:], 0.0, A.mult, A.add)
+    v("tt", f8(1), cnt, f8(0), A.mult)
+    v("tt", f8(2), f8(1), i8(1), A.add)
+    x_c1 = v("copy", T.cu1[:], f8(2), cross=True)
+
+    def quant_a(i):
+        return v("quant", T.aq[:, 128 * i:128 * i + 128], T.asc[:, 128 * i:128 * i + 128], T.at[:, 512 * i:512 * i + 512], deps=(ld_a,),
+                 cross=True)
+
+    x_a = [quant_a(0)]
     s_x1 = op("s", "act", (T.x1s[:], T.halls[:].indirect(T.cu1[:]), CP), [x_c1] + arrived)
     x_x1 = v("copy", T.x1[:].bitcast(dt.uint32), T.hall[:].bitcast(dt.uint32).indirect(T.cu1[:]), deps=[x_c1] + arrived, cross=True)
-    rows = []
-
-    def between1():
-        v("copy", T.base1[:], T.sc[:].indirect(T.cu1[:]), deps=("v", x_c1))
-        rows.append(v("copy", T.chr1[:], T.io1[:].indirect(T.cu1[:]), deps=(), cross=True))
-        v("tr", T.bt[:], T.base1[:])
-
-    update(T.hs1, T.h1, T.x1, T.x1s, T.e1t, ld_e1, (x_x1, s_x1, x_a), between1)
-    dma("y", T.ch[0:1, :], T.chr1[0:1, :], (rows[0],))
+    x_a += [quant_a(i) for i in (1, 2, 3)]
+    update(T.hs1, T.h1, T.x1, T.x1s, T.e1t, ld_e1, (x_x1, s_x1), x_a,
+           lambda: v("copy", T.base1[:], T.sc[:].indirect(T.cu1[:]), deps=("v", x_c1)))
     x_h1 = v("quant", T.h1q[:], T.h1s[:], T.h1[:], cross=True)
 
     m = op("t", "mm", (T.ps[:, 0:128], T.uq[:], T.us[:], T.h1q[:], T.h1s[:], True, True), (x_h1,))
-    v("quant", T.win2[:, 128:256], T.win2s[:, 128:256], T.h1[:], deps=())
+    x_off2 = v("copy", T.off2[:], T.l2[:], deps=(ld_l2,), cross=True)
+    s_kt = op("s", "act", (T.kt[:], T.io1[:].indirect(T.off2[:]), CP), (x_off2,), scale=1.0 / TOP)
+    v("tr", T.bt[:], T.base1[:])
     v("tr", T.gt[:], T.ps[:, 0:128], deps=(m,))
     x_sp = v("tt", T.sp[:, 4 * me:4 * me + 4], T.gt[:, 0:128:32], T.bt[:, 0:128:32], A.add, cross=True)
-    send("ae", lambda q: T.sp[:, 4 * me:4 * me + 4], lambda d: T.sp[:, 4 * me:4 * me + 4], (x_sp,))
+    own_sp = T.sp[:, 4 * me:4 * me + 4]
+    send(far(T, topo, core, me, SCORES, "ae", lambda q: own_sp, lambda d: own_sp), (x_sp,))
 
-    x_e0r = v("ts", T.e0r2[:], T.kt[:, 0:512:4], TOP, None, A.mult, deps=(s_kt,), cross=True)
-    b_e0 = op("g", "bc", (T.e0b2[:], T.e0r2[0:1, :], 128), (x_e0r,))
-    v("set", T.d1[:], 0.0, deps=())
-    v("set", T.hold32[:, 256:512], 1.0, deps=())
-    v("set", T.rst[:, 128:512], 0.0, deps=())
-    v("tt", T.key2[:], T.kt[:], T.eidx[:], A.add, deps=(s_e,))
+    v("quant", T.win2[:, 128:256], T.win2s[:, 128:256], T.h1[:], deps=())
     x_w = v("quant", T.wq[:], T.ws[:], T.wt[:], deps=(ld_w,), cross=True)
-    e0table(T.e0b2[:], ("v", b_e0))
-    v("set", T.hold32[:, 256:512:32], 0.0)
-    v("set", T.rst[:, 128:512:4], -1.0e29, deps=())
+    v("tt", T.key2[:], T.kt[:], T.eidx[:], A.add, deps=(s_kt, s_e))
 
     v("copy", T.d1[:, 0:512:32], T.sp[:, 0:16], deps=("v", "ae", x_sp))
     s_rp = op("s", "act", (T.rp[:, 512:1024], T.sp[:].indirect(T.repo[:]), CP), ("ae", x_sp, x_rep))
@@ -284,60 +331,85 @@ def rank_program(g, core, T, topo):
     s_g2 = op("s", "act", (T.gv[:, 256:512], T.sc2[:].indirect(T.off2[:, 16:32]), CP), (x_s2,))
     wait("v", (x_s3, s_g2))
     marks(512)
-    v("scan", T.st[:], T.pm[:], T.key2[:], 0.0, A.max, A.min)
-    x_z2 = v("ts", T.zi2[:], T.st[:, 3:512:4], TOP, None, A.mult, cross=True)
+    x_st = v("scan", T.st[:], T.pm[:], T.key2[:], 0.0, A.max, A.min, cross=True)
+    x_z2 = v("ts", T.zi2[:], T.st[:, 3:512:4], TOP, None, A.mult, deps=(x_st,), cross=True)
+    s_zr = op("s", "act", (T.zrow[0:1, :], T.st[0:1, 3:512:4], CP), (x_st,))
     b_z = op("g", "bc", (T.zb2[:], T.zi2[0:1, :], 128), (x_z2,))
+    b_zf = op("g", "bc", (T.zf2[:], T.zrow[0:1, :], 128), (s_zr,))
     v("ts", T.am[:], T.zi2[:], 896, None, A.bitwise_and, deps=(x_z2,))
     v("ts", T.mb[:, 1:129], T.am[:], float(128 * me), None, A.is_equal)
     v("scan", T.ce[:], T.ones[:], T.mb[:, 0:128], 0.0, A.mult, A.add)
     v("ts", T.pp[:], T.ce[:], T.ip[:], None, A.is_le)
     v("scan", T.ks[:], T.pp[:], T.st[:, 3:512:4], 0.0, A.max, A.min)
     v("ts", T.lr[:], T.mask16[:, 0:32], T.ks[:, 127:128], None, A.mult)
+    x_sj = v("ts", T.sj[:], T.zb2[:], 7, 7, A.logical_shift_right, A.bitwise_and, deps=(b_z,), cross=True)
     v("tr", T.lt[:], T.lr[:])
+    x_mk = v("ts", T.mk[:], T.sj[:], T.spart[:], None, A.is_equal, deps=(x_sj,), cross=True)
     x_ls = v("scan", T.ls[:], T.hold16[:, 0:32], T.lt[:], 0.0, A.mult, A.add, cross=True)
-    s_r8 = quarters(lambda a, b: T.r8[32 * b:32 * b + 32, 2 * a:2 * a + 2], lambda a: T.ls[32 * a:32 * a + 32, 15:32:16], x_ls)
+    x_cum = v("scan", T.cum[:], T.ones[:], T.mk[:], 0.0, A.mult, A.add, deps=(x_mk,), cross=True)
+    s_r8 = fresh()
+    for i in range(16):
+        a, b = i % 4, i // 4
+        out, src = T.r8[32 * b:32 * b + 32, 2 * a:2 * a + 2], T.ls[32 * a:32 * a + 32, 15:32:16]
+        if i < 10:
+            v("copy", out, src, deps=(x_ls,))
+        else:
+            op("s", "act", (out, src, CP), (x_ls,), sem=s_r8)
+    s_mk = op("s", "act", (T.dup2[:], T.mk[:].indirect(T.dupo[:]), CP), (x_mk,))
     v("ts", T.r8i[:], T.r8[:], TOP, None, A.mult, deps=("v", s_r8))
+    x_cs = v("scan", T.cs[:], T.mask16[:], T.zf2[:], 0.0, A.max, A.min, deps=(b_zf,), cross=True)
     v("ts", T.r8n[:], T.r8i[:], 127, None, A.bitwise_and)
+    x_i0 = v("ts", i8(0), T.cs[:, 15:128:16], TOP, None, A.mult, deps=(x_cs,), cross=True)
     x_of = v("copy", T.offp[:], T.r8n[:], cross=True)
+    x_i2 = v("ts", i8(2), i8(0), 1023, None, A.bitwise_and, deps=(x_i0,), cross=True)
     s_pk = op("s", "act", (T.pks[:], T.h1s[:].indirect(T.offp[:]), CP), (x_of, x_h1))
     x_pk = v("copy", T.pk[:].bitcast(dt.uint32), T.h1q[:].bitcast(dt.uint32).indirect(T.offp[:]), deps=(x_of, x_h1), cross=True)
-    land = slice(16 * me, 16 * me + 16)
-    send("a2", lambda q: T.pk[:, 16 * q:16 * q + 16].bitcast(dt.uint8), lambda d: T.win2[:, land].bitcast(dt.uint8), (x_pk,))
-    send("a2", lambda q: T.pks[:, 16 * q:16 * q + 16], lambda d: T.win2s[:, land], (s_pk,))
 
-    v("ts", T.sj[:], T.zb2[:], 7, 7, A.logical_shift_right, A.bitwise_and, deps=(b_z,))
-    v("ts", T.cj[:], T.zb2[:], 1023, None, A.bitwise_and, deps=())
-    v("ts", T.mk[:], T.sj[:], T.spart[:], None, A.is_equal)
-    cnt, ctab = T.vs[:, 31:256:32], T.cs[:, 15:128:16]
-    capacity(T.mk[:], (ctab, ()), ("v",), lambda: v("tt", T.cw[:], T.cj[:], T.mask16[:], A.mult, deps=()))
-    x_c2 = v("copy", T.cu2[:], T.cf[:], cross=True)
-    v("copy", T.ti[:], ctab, deps=())
-    v("ts", T.isr[:], cnt, 0.5, None, A.is_gt, deps=())
-    v("ts", T.own[:], T.cf[:], float(128 - 128 * me), None, A.add, deps=())
-    v("ts", T.tsh[:], T.ti[:], 7, None, A.logical_shift_right)
-    v("tt", T.isk[:], T.isr[:], T.ov[:], A.subtract, deps=())
-    v("ts", T.t1[:], T.tsh[:], 16.0, -1.0, A.mult, A.add)
-    v("tt", T.t2[:], T.t1[:], cnt, A.add)
-    v("tt", T.dd[:], T.t2[:], T.own[:], A.subtract)
-    v("tt", T.de[:], T.dd[:], T.isk[:], A.mult)
-    v("tt", T.ix[:], T.de[:], T.own[:], A.add)
-    x_ix = v("copy", T.ixu[:], T.ix[:], cross=True)
+    runs = [slice(16 * min(share), 16 * max(share) + 16) for share in PICKS_H]
+    send(near(T, topo, core, me, "kc", lambda i: T.pk[:, runs[i]].bitcast(dt.uint8)), (x_pk,))
+    send(near(T, topo, core, me, "ks", lambda i: T.pks[:, runs[i]]), (s_pk,))
+    for sem, src, dst in pick_calls(T, me):
+        send(far(T, topo, core, me, PICKS, "a2", src, dst), ())
+
+    base = float(128 - 128 * me)
+    v("tt", T.v2[:], T.cum[:].indirect(T.dupo[:]), T.dup2[:], A.mult, deps=(x_cum, s_mk))
+    v("ts", f8(4), i8(2), base, None, A.add, deps=(x_i2,))
+    x_i3 = v("ts", i8(3), i8(2), 7, None, A.logical_shift_right, deps=(), cross=True)
+    v("tr", T.vt[:], T.v2[:])
+    v("tt", f8(5), etab2, i8(2), A.subtract, deps=())
+    v("ts", f8(6), i8(3), 16.0, -1.0, A.mult, A.add, deps=(x_i3,))
+    v("scan", T.vs[:], T.hold32[:, 0:256], T.vt[:], 0.0, A.mult, A.add)
+    x_f7 = v("tt", f8(7), f8(6), f8(4), A.subtract, deps=(), cross=True)
+    v("ts", f8(8), cnt, 16.5, None, A.is_gt)
+    v("ts", f8(9), cnt, 0.5, None, A.is_gt, deps=())
+    v("tt", f8(10), f8(7), cnt, A.add, deps=(x_f7,))
+    v("tt", f8(12), f8(8), f8(5), A.mult)
+    v("tt", f8(11), f8(9), f8(8), A.subtract, deps=())
+    v("tt", f8(14), f8(12), f8(4), A.add)
+    v("tt", f8(13), f8(11), f8(10), A.mult, deps=())
+    v("tt", f8(15), f8(13), f8(14), A.add)
+    x_ix = v("copy", T.ixu[:], f8(15), cross=True)
+    v("tt", f8(16), f8(12), i8(2), A.add, deps=())
     s_x2 = op("s", "act", (T.x2s[:], T.win2s[:].indirect(T.ixu[:]), CP), (x_ix, "a2"))
+    x_c2 = v("copy", T.cu2[:], f8(16), cross=True)
     x_x2 = v("copy", T.x2[:].bitcast(dt.uint32), T.win2[:].bitcast(dt.uint32).indirect(T.ixu[:]), deps=(x_ix, "a2"), cross=True)
+    rows = []
 
     def between2():
         v("copy", T.base2[:], T.sc2[:].indirect(T.cu2[:]), deps=("v", x_c2))
-        rows.append(v("copy", T.chr2[:], T.io1[:].indirect(T.cu2[:]), deps=(), cross=True))
+        rows.append(v("copy", T.chr1[:], T.io1[:].indirect(T.cu1[:]), deps=(), cross=True))
 
-    update(T.hs2, T.h2, T.x2, T.x2s, T.e2t, ld_e2, (x_x2, s_x2, x_a), between2)
-    dma("y", T.ch[1:2, :], T.chr2[0:1, :], (rows[1],))
+    update(T.hs2, T.h2, T.x2, T.x2s, T.e2t, ld_e2, (x_x2, s_x2), x_a, between2)
+    dma("y", T.ch[0:1, :], T.chr1[0:1, :], (rows[0],))
     x_h2 = v("quant", T.h2q[:], T.h2s[:], T.h2[:], cross=True)
+    x_ch2 = v("copy", T.chr2[:], T.io1[:].indirect(T.cu2[:]), deps=(), cross=True)
 
     m_y = op("t", "mm", (T.ps[:, 512:640], T.wq[:], T.ws[:], T.h2q[:], T.h2s[:], True, True), (x_h2, x_w))
     m_g = op("t", "mm", (T.ps[:, 0:128], T.uq[:], T.us[:], T.h2q[:], T.h2s[:], True, True), (x_h2,))
     dma("y", T.oc[:], T.h2q[:].bitcast(dt.uint8), (x_h2,))
     for k in range(4):
         dma("ys"[k // 2], T.osc[4 * k:4 * k + 4, :], T.h2s[32 * k:32 * k + 4, :], (x_h2,))
+    dma("y", T.ch[1:2, :], T.chr2[0:1, :], (x_ch2,))
     s_y = op("s", "act", (T.yt[:], T.ps[:, 512:640], CP), (m_y,))
     x_g = v("tt", T.gout[:], T.ps[:, 0:128], T.base2[:], A.add, deps=("v", m_g), cross=True)
     dma("s", T.y[:], T.yt[:], (s_y,))

@@ -21,7 +21,7 @@ SCRATCH = {
     "h2q": _sb(128, X4), "h2s": _sb(128, U8),
     "ones": _sb(128, B), "hold32": _sb(512, B), "hold16": _sb(128, B), "rst": _sb(512, F), "pidx": _sb(1, I), "r15": _sb(1, I),
     "r31": _sb(1, I), "ip": _sb(1, F), "sp31": _sb(1, F), "spx": _sb(1, F), "spart": _sb(1, F), "cmod": _sb(128, I),
-    "mask16": _sb(128, B), "ci": _sb(128, I), "repo": _sb(32, U16), "rsh": _sb(32, I), "dupo": _sb(16, U16),
+    "mask16": _sb(128, B), "ci": _sb(128, I), "repo": _sb(40, U16), "rsh": _sb(40, I), "dupo": _sb(16, U16),
     "io1": _sb(1024, F), "eidx": _sb(512, F),
     "off1": _sb(32, U16), "offo": _sb(32, U16), "offh": _sb(16, U16), "off2": _sb(32, U16), "er": _sb(512, F), "er2": _sb(512, F),
     "kt": _sb(512, F), "kp": _sb(256, F), "key1": _sb(256, F), "key2": _sb(512, F), "st1": _sb(256, F),
@@ -34,19 +34,20 @@ SCRATCH = {
     "base1": _sb(128, F), "bt": _sb(128, F), "gt": _sb(128, F), "sp": _sb(32, F), "d1": _sb(512, F), "rp": _sb(1024, F),
     "sc2": _sb(1024, F), "base2": _sb(128, F), "gout": _sb(128, F), "yt": _sb(128, F),
     "am": _sb(128, I), "mb": _sb(144, B), "ce": _sb(128, B), "pp": _sb(128, B), "ks": _sb(128, F), "lr": _sb(32, F),
-    "lt": _sb(32, F), "ls": _sb(32, F), "r8": _sb(8, F), "r8i": _sb(8, I), "r8n": _sb(8, I), "offp": _sb(8, U16),
+    "lt": _sb(32, F), "ls": _sb(128, F), "r8i": _sb(8, I), "r8n": _sb(8, I), "offp": _sb(8, U16),
     "ixu": _sb(8, U16), "chr1": _sb(128, F), "chr2": _sb(128, F),
     "hs1": _sb(512, F), "hs2": _sb(512, F), "h1": _sb(512, B), "h2": _sb(512, B),
     "ps": ("psum", [128, 2048], F), "pr": ("psum", [128, 2048], F),
 }
 
-REMOTE = ["al", "a0a", "a0b", "a0c", "ae", "a2", "left", "hl", "kc", "ks"]
-SEMAPHORES = REMOTE + ["v"] + ["s%d" % i for i in range(135)]
+REMOTE = ["al", "a0a", "a0b", "a0h", "ae", "a2", "left", "hl", "hc", "kc", "ks"]
+SEMAPHORES = REMOTE + ["v"] + ["s%d" % i for i in range(138)]
 A = AluOpType
 CP, IDN = ActivationFunctionType.Copy, ActivationFunctionType.Identity
 TOP = 2.0 ** 19
 
-TIERS = (("a0a", {1: 2, 2: 2, 3: 2, 4: 2}), ("a0b", {5: 4, 6: 4}), ("a0c", {7: 8}))
+TIERS = (("a0a", {1: 2, 2: 2, 3: 2, 4: 2}), ("a0b", {5: 4, 6: 4}))
+TIER_H = ("a0h", {7: 8})
 LISTS = ({1: 2, 2: 2, 3: 2, 4: 2}, {5: 2, 6: 2, 7: 4})
 SCORES = {q: 1 for q in range(1, 8)}
 PICKS, PICKS_H = {1: 2, 2: 2, 3: 4}, ({4: 4, 5: 4}, {6: 4, 7: 4})
@@ -75,12 +76,20 @@ def far(T, topo, core, me, share, sem, src, dst):
     return parts
 
 
-def near(T, topo, core, me, sem, src):
-    hp = helpers(core, topo)
+def inner(T, topo, core, me):
     away = topo.engines(core, T.cores[(me + 1) % len(T.cores)])
-    e = [x for x in topo.engines(core, hp[0]) if x not in away]
-    n = len(e) // len(hp)
-    return [(c, e[n * i:n * i + n], sem, src(i), src(i)) for i, c in enumerate(hp)]
+    return [x for x in topo.engines(core, helpers(core, topo)[0]) if x not in away]
+
+
+def near(T, topo, core, me, sem, src, n=None):
+    hp, e = helpers(core, topo), inner(T, topo, core, me)
+    m = len(e) // len(hp)
+    return [(c, e[m * i:m * i + (n or m)], sem, src(i), src(i)) for i, c in enumerate(hp)]
+
+
+def columns0(T, me):
+    mine = slice(128 * me, 128 * me + 128)
+    return T.hall[:, mine].bitcast(dt.uint8), T.halls[:, mine]
 
 
 def pick_calls(T, me):
@@ -90,10 +99,13 @@ def pick_calls(T, me):
 
 
 def helper_program(g, core, T, topo, me, k):
-    N = len(T.cores)
-    n = len(near(T, topo, T.cores[me], me, "hl", lambda i: None)[k][1])
-    g.wait_ge(T.sem.hl, n)
+    N, own = len(T.cores), T.cores[me]
+    g.wait_ge(T.sem.hl, 1)
     left = fused(g, T, topo, core, far(T, topo, core, me, LISTS[k], "al", lambda q: T.pst[:], lambda d: T.pl[(me - d) % N]))
+    g.wait_ge(T.sem.hc, len(inner(T, topo, own, me)))
+    piece = columns0(T, me)[k]
+    left += fused(g, T, topo, core, far(T, topo, core, me, TIER_H[1], TIER_H[0], lambda q: piece, lambda d: piece))
+    n = len(near(T, topo, own, me, "kc", lambda i: None)[k][1])
     for sem, src, dst in pick_calls(T, me):
         g.wait_ge(T.sem[sem], n)
         left += fused(g, T, topo, core, far(T, topo, core, me, PICKS_H[k], "a2", src, dst))
@@ -141,8 +153,8 @@ def rank_program(g, core, T, topo):
         wait(q, deps)
         return mark(q, F_[name](*args, **kw), 1, cross, sem)
 
-    def v(name, *args, deps=("v",), cross=False):
-        return op("v", name, args, deps, cross)
+    def v(name, *args, deps=("v",), cross=False, sem=None):
+        return op("v", name, args, deps, cross, sem)
 
     def send(parts, deps):
         wait("g", deps)
@@ -152,10 +164,12 @@ def rank_program(g, core, T, topo):
         return sum(n for share in shares for n in share.values())
 
     total["al"], total["ae"], total["a2"] = count(*LISTS), count(SCORES), 2 * count(PICKS, *PICKS_H)
-    for sem, share in TIERS:
+    for sem, share in TIERS + (TIER_H,):
         total[sem] = 2 * count(share)
-    arrivals = [sem for sem, share in TIERS]
+    arrivals = [sem for sem, share in TIERS + (TIER_H,)]
     mine = slice(128 * me, 128 * me + 128)
+    halves = slice(0, 64), slice(64, 128)
+    two = {name: (fresh(), fresh()) for name in ("scan", "mark", "key", "whole", "rank")}
 
     ld_e0 = dma("y", T.e0t[:], T.e0[:])
     ld_ps = dma("s", T.pst[:], T.p2[:])
@@ -179,19 +193,22 @@ def rank_program(g, core, T, topo):
     i_1 = fresh()
     for k in range(1, 8):
         op("s", "act", (T.io1[:, 128 * k:128 * k + 128], T.io1[:, 0:128], IDN), (i_0,), sem=i_1, bias=float(128 * k))
+
+    send(near(T, topo, core, me, "hl", lambda i: T.pst[:], 1), (ld_ps,))
+    x_h0 = v("quant", T.hall[:, mine], T.halls[:, mine], T.e0t[:], deps=(ld_e0,), cross=True)
+    for sem, share in TIERS:
+        if sem == TIERS[1][0]:
+            for c, piece in zip(helpers(core, topo), columns0(T, me)):
+                send([(c, inner(T, topo, core, me), "hc", piece, piece)], (x_h0,))
+        for piece in columns0(T, me):
+            send(far(T, topo, core, me, share, sem, lambda q: piece, lambda d: piece), (x_h0,))
+
     v("set", T.ones[:], 1.0)
     v("ts", T.r15[:], T.pidx[:], 15, None, A.bitwise_and, deps=(i_p,))
     v("ts", T.r31[:], T.pidx[:], 31, None, A.bitwise_and, deps=())
     v("copy", T.ci[:], T.io1[:, 0:128], deps=(i_0,))
     for buf, c in ((T.hold32[:, 0:256], 1.0), (T.hold16[:], 1.0), (T.rst[:, 0:256], 0.0), (T.pm[:, 0:512:4], 1.0), (T.mb[:, 0:1], 0.0)):
         v("set", buf, c, deps=())
-
-    x_h0 = v("quant", T.hall[:, mine], T.halls[:, mine], T.e0t[:], deps=(ld_e0,), cross=True)
-    for sem, share in TIERS:
-        for piece in (T.hall[:, mine].bitcast(dt.uint8), T.halls[:, mine]):
-            send(far(T, topo, core, me, share, sem, lambda q: piece, lambda d: piece), (x_h0,))
-    send(near(T, topo, core, me, "hl", lambda i: T.pst[:]), (ld_ps,))
-
     s_e = op("s", "act", (T.eidx[:], T.io1[:, 0:512], CP), (i_1,), scale=1024.0 / TOP)
 
     for a in range(2):
@@ -208,11 +225,11 @@ def rank_program(g, core, T, topo):
     v("set", T.rst[:, 0:256:4], -1.0e29, deps=())
     v("copy", T.sp31[:], T.r31[:], deps=())
     v("ts", T.cmod[:], T.ci[:], 15, None, A.bitwise_and, deps=())
-    v("ts", T.rsh[:], T.ci[:, 0:32], 1, None, A.logical_shift_right, deps=())
+    v("ts", T.rsh[:], T.ci[:, 0:40], 1, None, A.logical_shift_right, deps=())
     v("ts", T.spx[:], T.sp31[:], float(me), 99.0, A.is_equal, A.mult, deps=("v", x_off1))
     v("ts", T.mask16[:], T.cmod[:], T.ip[:], None, A.is_equal, deps=())
     v("ts", T.dupo[:], T.rsh[:, 0:16], 16.0, T.ip[:], A.mult, A.add, deps=())
-    x_rep = v("ts", T.repo[:], T.rsh[:], 16.0, None, A.add, deps=(), cross=True)
+    x_rep = v("ts", T.repo[:], T.rsh[:], 12.0, None, A.add, deps=(), cross=True)
     v("tt", T.spart[:], T.spx[:], T.sp31[:], A.add)
     for a in range(2):
         h = slice(64 * a, 64 * a + 64)
@@ -233,7 +250,7 @@ def rank_program(g, core, T, topo):
     e0table(T.ew2, T.es2, T.er2, ("v", s_er2))
 
     sc_done = []
-    order = [(me, x_h0)] + [((me - q) % N, sem) for sem, share in TIERS for q in share]
+    order = [(me, x_h0)] + [((me - q) % N, sem) for sem, share in (TIERS[0], TIER_H, TIERS[1]) for q in share]
     for i, (r, sem) in enumerate(order):
         cs = slice(128 * r, 128 * r + 128)
         bank = (T.ps if i < 4 else T.pr)[:, 512 * (i % 4):512 * (i % 4) + 128]
@@ -244,10 +261,19 @@ def rank_program(g, core, T, topo):
             sc_done.append(op("s", "act", (T.sc[:, cs], bank, CP), (m,)))
     arrived = [x_h0] + arrivals
 
-    def marks(w):
-        v("scan", T.mx[:, 0:w], T.rst[:, 0:w], T.gv[:, 0:w], 0.0, A.add, A.max)
-        for k in (1, 2, 3):
-            v("tt", T.pm[:, k:w:4], T.gv[:, k:w:4], T.mx[:, k - 1:w:4], A.is_gt, deps=("v",) if k == 1 else ())
+    def choose(w, parts, key, st):
+        h = w // 2
+        for i in range(2):
+            c = slice(h * i, h * i + h)
+            v("scan", T.mx[:, c], T.rst[:, c], T.gv[:, c], 0.0, A.add, A.max, deps=(parts[i],), sem=two["scan"][i])
+        for i in range(2):
+            for k in (1, 2, 3):
+                a, e = h * i + k, h * i + h
+                v("tt", T.pm[:, a:e:4], T.gv[:, a:e:4], T.mx[:, a - 1:e:4], A.is_gt, deps=(two["scan"][i],), sem=two["mark"][i])
+        for i in range(2):
+            c = slice(h * i, h * i + h)
+            v("scan", st[:, c], T.pm[:, c], key[:, c], 0.0, A.max, A.min, deps=(two["mark"][i],), sem=two["key"][i])
+        return two["key"]
 
     def f8(i):
         return T.f8[:, 8 * i:8 * i + 8]
@@ -257,60 +283,61 @@ def rank_program(g, core, T, topo):
 
     etab, etab2, cnt = T.es[:, 15:128:16], T.es2[:, 15:128:16], T.vs[:, 31:256:32]
 
-    def update(hs, h, X, Xs, e, ld_e, deps, x_a, between):
+    def quant_a(i):
+        return v("quant", T.aq[:, 128 * i:128 * i + 128], T.asc[:, 128 * i:128 * i + 128], T.at[:, 512 * i:512 * i + 512], deps=(ld_a,),
+                 cross=True)
+
+    def update(hs, h, X, Xs, e, ld_e, deps, x_a, between=None):
         dep = []
         for i in range(4):
             s = slice(128 * i, 128 * i + 128)
             m = op("t", "mm", (T.pr[:, 512 * i:512 * i + 128], T.aq[:, s], T.asc[:, s], X[:], Xs[:], True, True), tuple(deps) + (x_a[i],))
             dep.append(op("s", "act", (hs[:, s], T.pr[:, 512 * i:512 * i + 128], CP), (m,), scale=0.05))
-        between()
+        if between:
+            between()
         for i in range(4):
             v("tt", h[:, i:512:4], hs[:, 128 * i:128 * i + 128], e[:, i:512:4], A.add, deps=(dep[i], ld_e))
 
-    v("copy", T.gv[:, 0:128], T.sc[:].indirect(T.offh[:, 0:8]), deps=["v"] + sc_done)
+    x_g1 = v("copy", T.gv[:, 0:128], T.sc[:].indirect(T.offh[:, 0:8]), deps=["v"] + sc_done, cross=True)
     s_g1 = op("s", "act", (T.gv[:, 128:256], T.sc[:].indirect(T.offh[:, 8:16]), CP), sc_done)
-    wait("v", ("v", s_g1))
-    marks(256)
-    x_st1 = v("scan", T.st1[:], T.pm[:, 0:256], T.key1[:], 0.0, A.max, A.min, cross=True)
+    x_st1 = choose(256, (x_g1, s_g1), T.key1, T.st1)
     s_zf = fresh()
-    for b in range(2):
-        for a in range(2):
-            here, there, to = slice(64 * a, 64 * a + 64), slice(64 * b, 64 * b + 64), slice(64 * a, 64 * a + 64)
-            v("ts", T.zb1[there, to], T.st1[here, 3:256:4], TOP, None, A.mult, deps=(x_st1,))
-            op("s", "act", (T.zf1[there, to], T.st1[here, 3:256:4], CP), (x_st1,), sem=s_zf)
+    for a, to in enumerate(halves):
+        for there in halves:
+            v("ts", T.zb1[there, to], T.st1[to, 3:256:4], TOP, None, A.mult, deps=x_st1, sem=two["whole"][a])
+            op("s", "act", (T.zf1[there, to], T.st1[to, 3:256:4], CP), x_st1, sem=s_zf)
 
-    v("ts", T.sj[:], T.zb1[:], 7, 7, A.logical_shift_right, A.bitwise_and)
-    x_th = v("ts", T.th[:], T.sj[:], T.spart[:], 1.0e6, A.not_equal, A.mult, cross=True)
+    for i, c in enumerate(halves):
+        v("ts", T.sj[:, c], T.zb1[:, c], 7, 7, A.logical_shift_right, A.bitwise_and, deps=(two["whole"][i],), sem=two["rank"][i])
+    x_th = fresh()
+    for i, c in enumerate(halves):
+        v("ts", T.th[:, c], T.sj[:, c], T.spart[:], 1.0e6, A.not_equal, A.mult, deps=(two["rank"][i],), sem=x_th)
     s_th = op("s", "act", (T.dup1[:], T.th[:].indirect(T.dupo[:]), CP), (x_th,))
     v("ts", T.mk[:], T.sj[:], T.spart[:], None, A.is_equal, deps=())
-    v("scan", T.cum[:], T.ones[:], T.mk[:], -16.5, A.mult, A.add)
-    v("scan", T.cs[:], T.mask16[:], T.zf1[:], 0.0, A.max, A.min, deps=(s_zf,))
-    v("ts", i8(0), T.cs[:, 15:128:16], TOP, None, A.mult)
-    v("ts", i8(1), i8(0), 1023, None, A.bitwise_and)
-    v("tt", T.v2[:], T.cum[:].indirect(T.dupo[:]), T.dup1[:], A.is_gt, deps=("v", s_th))
-    v("tt", f8(0), etab, i8(1), A.subtract, deps=())
-    v("tr", T.vt[:], T.v2[:])
-    v("scan", T.vs[:], T.hold32[:, 0:256], T.vt[:], 0.0, A.mult, A.add)
+    x_cum1 = v("scan", T.cum[:], T.ones[:], T.mk[:], -16.5, A.mult, A.add, cross=True)
+    x_cs1 = v("scan", T.cs[:], T.mask16[:], T.zf1[:], 0.0, A.max, A.min, deps=(s_zf,), cross=True)
+    x_a = [quant_a(0)]
+    x_v1 = v("tt", T.v2[:], T.cum[:].indirect(T.dupo[:]), T.dup1[:], A.is_gt, deps=(x_cum1, s_th), cross=True)
+    x_i0 = v("ts", i8(0), T.cs[:, 15:128:16], TOP, None, A.mult, deps=(x_cs1,), cross=True)
+    x_vt = v("tr", T.vt[:], T.v2[:], deps=(x_v1,), cross=True)
+    x_i1 = v("ts", i8(1), i8(0), 1023, None, A.bitwise_and, deps=(x_i0,), cross=True)
+    v("scan", T.vs[:], T.hold32[:, 0:256], T.vt[:], 0.0, A.mult, A.add, deps=(x_vt,))
+    v("tt", f8(0), etab, i8(1), A.subtract, deps=(x_i1,))
     v("tt", f8(1), cnt, f8(0), A.mult)
     v("tt", f8(2), f8(1), i8(1), A.add)
     x_c1 = v("copy", T.cu1[:], f8(2), cross=True)
 
-    def quant_a(i):
-        return v("quant", T.aq[:, 128 * i:128 * i + 128], T.asc[:, 128 * i:128 * i + 128], T.at[:, 512 * i:512 * i + 512], deps=(ld_a,),
-                 cross=True)
-
-    x_a = [quant_a(0)]
     s_x1 = op("s", "act", (T.x1s[:], T.halls[:].indirect(T.cu1[:]), CP), [x_c1] + arrived)
+    s_b1 = op("s", "act", (T.base1[:], T.sc[:].indirect(T.cu1[:]), CP))
     x_x1 = v("copy", T.x1[:].bitcast(dt.uint32), T.hall[:].bitcast(dt.uint32).indirect(T.cu1[:]), deps=[x_c1] + arrived, cross=True)
     x_a += [quant_a(i) for i in (1, 2, 3)]
-    update(T.hs1, T.h1, T.x1, T.x1s, T.e1t, ld_e1, (x_x1, s_x1), x_a,
-           lambda: v("copy", T.base1[:], T.sc[:].indirect(T.cu1[:]), deps=("v", x_c1)))
+    update(T.hs1, T.h1, T.x1, T.x1s, T.e1t, ld_e1, (x_x1, s_x1), x_a)
     x_h1 = v("quant", T.h1q[:], T.h1s[:], T.h1[:], cross=True)
 
     m = op("t", "mm", (T.ps[:, 0:128], T.uq[:], T.us[:], T.h1q[:], T.h1s[:], True, True), (x_h1,))
     x_off2 = v("copy", T.off2[:], T.l2[:], deps=(ld_l2,), cross=True)
     s_kt = op("s", "act", (T.kt[:], T.io1[:].indirect(T.off2[:]), CP), (x_off2,), scale=1.0 / TOP)
-    v("tr", T.bt[:], T.base1[:])
+    v("tr", T.bt[:], T.base1[:], deps=(s_b1,))
     v("tr", T.gt[:], T.ps[:, 0:128], deps=(m,))
     x_sp = v("tt", T.sp[:, 4 * me:4 * me + 4], T.gt[:, 0:128:32], T.bt[:, 0:128:32], A.add, cross=True)
     own_sp = T.sp[:, 4 * me:4 * me + 4]
@@ -319,25 +346,33 @@ def rank_program(g, core, T, topo):
     v("quant", T.win2[:, 128:256], T.win2s[:, 128:256], T.h1[:], deps=())
     x_w = v("quant", T.wq[:], T.ws[:], T.wt[:], deps=(ld_w,), cross=True)
     v("tt", T.key2[:], T.kt[:], T.eidx[:], A.add, deps=(s_kt, s_e))
+    x_ch1 = v("copy", T.chr1[:], T.io1[:].indirect(T.cu1[:]), deps=(x_c1, i_1), cross=True)
+    dma("y", T.ch[0:1, :], T.chr1[0:1, :], (x_ch1,))
 
-    v("copy", T.d1[:, 0:512:32], T.sp[:, 0:16], deps=("v", "ae", x_sp))
-    s_rp = op("s", "act", (T.rp[:, 512:1024], T.sp[:].indirect(T.repo[:]), CP), ("ae", x_sp, x_rep))
-    v("scan", T.rp[:, 0:512], T.hold32[:], T.d1[:], 0.0, A.mult, A.add)
-    v("tr", T.sc2[:, 0:512], T.rp[:, 0:512])
-    x_s2 = v("tr", T.sc2[:, 512:1024], T.rp[:, 512:1024], deps=(s_rp,), cross=True)
+    v("copy", T.d1[:, 0:384:32], T.sp[:, 0:12], deps=("v", "ae", x_sp))
+    s_rp = [op("s", "act", (T.rp[:, 384:640], T.sp[:].indirect(T.repo[:, 0:16]), CP), ("ae", x_sp, x_rep)),
+            op("s", "act", (T.rp[:, 640:1024], T.sp[:].indirect(T.repo[:, 16:40]), CP))]
+    parts = slice(0, 192), slice(192, 384)
+    for i, c in enumerate(parts):
+        v("scan", T.rp[:, c], T.hold32[:, c], T.d1[:, c], 0.0, A.mult, A.add, deps=("v",) if i == 0 else (), sem=two["scan"][i])
+    for i, c in enumerate(parts):
+        v("tr", T.sc2[:, c], T.rp[:, c], deps=(two["scan"][i],))
+    v("tr", T.sc2[:, 384:640], T.rp[:, 384:640], deps=(s_rp[0],))
+    x_s2 = v("tr", T.sc2[:, 640:1024], T.rp[:, 640:1024], deps=(s_rp[1],), cross=True)
 
     wait("v", ("v", x_s2))
-    x_s3 = v("copy", T.gv[:, 0:256], T.sc2[:].indirect(T.off2[:, 0:16]), deps=())
+    x_s3 = v("copy", T.gv[:, 0:256], T.sc2[:].indirect(T.off2[:, 0:16]), deps=(), cross=True)
     s_g2 = op("s", "act", (T.gv[:, 256:512], T.sc2[:].indirect(T.off2[:, 16:32]), CP), (x_s2,))
-    wait("v", (x_s3, s_g2))
-    marks(512)
-    x_st = v("scan", T.st[:], T.pm[:], T.key2[:], 0.0, A.max, A.min, cross=True)
-    x_z2 = v("ts", T.zi2[:], T.st[:, 3:512:4], TOP, None, A.mult, deps=(x_st,), cross=True)
-    s_zr = op("s", "act", (T.zrow[0:1, :], T.st[0:1, 3:512:4], CP), (x_st,))
-    b_z = op("g", "bc", (T.zb2[:], T.zi2[0:1, :], 128), (x_z2,))
+    x_st = choose(512, (x_s3, s_g2), T.key2, T.st)
+    for i, c in enumerate(halves):
+        v("ts", T.zi2[:, c], T.st[:, 256 * i + 3:256 * i + 256:4], TOP, None, A.mult, deps=(x_st[i],), sem=two["whole"][i])
+    s_zr = op("s", "act", (T.zrow[0:1, :], T.st[0:1, 3:512:4], CP), x_st)
+    b_z = op("g", "bc", (T.zb2[:], T.zi2[0:1, :], 128), two["whole"])
     b_zf = op("g", "bc", (T.zf2[:], T.zrow[0:1, :], 128), (s_zr,))
-    v("ts", T.am[:], T.zi2[:], 896, None, A.bitwise_and, deps=(x_z2,))
-    v("ts", T.mb[:, 1:129], T.am[:], float(128 * me), None, A.is_equal)
+    for i, c in enumerate(halves):
+        v("ts", T.am[:, c], T.zi2[:, c], 896, None, A.bitwise_and, deps=(two["whole"][i],), sem=two["rank"][i])
+    for i, c in enumerate(halves):
+        v("ts", T.mb[:, 64 * i + 1:64 * i + 65], T.am[:, c], float(128 * me), None, A.is_equal, deps=(two["rank"][i],))
     v("scan", T.ce[:], T.ones[:], T.mb[:, 0:128], 0.0, A.mult, A.add)
     v("ts", T.pp[:], T.ce[:], T.ip[:], None, A.is_le)
     v("scan", T.ks[:], T.pp[:], T.st[:, 3:512:4], 0.0, A.max, A.min)
@@ -345,19 +380,22 @@ def rank_program(g, core, T, topo):
     x_sj = v("ts", T.sj[:], T.zb2[:], 7, 7, A.logical_shift_right, A.bitwise_and, deps=(b_z,), cross=True)
     v("tr", T.lt[:], T.lr[:])
     x_mk = v("ts", T.mk[:], T.sj[:], T.spart[:], None, A.is_equal, deps=(x_sj,), cross=True)
-    x_ls = v("scan", T.ls[:], T.hold16[:, 0:32], T.lt[:], 0.0, A.mult, A.add, cross=True)
+    x_ls, x_r8, s_r8 = fresh(), fresh(), fresh()
+    for a in range(4):
+        qa = slice(32 * a, 32 * a + 32)
+        v("scan", T.ls[qa, qa], T.hold16[qa, 0:32], T.lt[qa, :], 0.0, A.mult, A.add, deps=("v",) if a == 0 else (), sem=x_ls)
     x_cum = v("scan", T.cum[:], T.ones[:], T.mk[:], 0.0, A.mult, A.add, deps=(x_mk,), cross=True)
-    s_r8 = fresh()
-    for i in range(16):
-        a, b = i % 4, i // 4
-        out, src = T.r8[32 * b:32 * b + 32, 2 * a:2 * a + 2], T.ls[32 * a:32 * a + 32, 15:32:16]
-        if i < 10:
-            v("copy", out, src, deps=(x_ls,))
+    for a, b in ((0, 1), (1, 0), (2, 3), (3, 2)):
+        out, src = [T.ls[32 * c:32 * c + 32, 32 * a + 15:32 * a + 32:16] for c in (b, a)]
+        if a < 2:
+            v("copy", out, src, deps=(x_ls,), sem=x_r8)
         else:
             op("s", "act", (out, src, CP), (x_ls,), sem=s_r8)
+    s_r9 = op("s", "act", (T.ls[64:128, 15:64:16], T.ls[0:64, 15:64:16], CP), (x_r8,))
+    v("copy", T.ls[0:64, 79:128:16], T.ls[64:128, 79:128:16], deps=(s_r8,))
     s_mk = op("s", "act", (T.dup2[:], T.mk[:].indirect(T.dupo[:]), CP), (x_mk,))
-    v("ts", T.r8i[:], T.r8[:], TOP, None, A.mult, deps=("v", s_r8))
     x_cs = v("scan", T.cs[:], T.mask16[:], T.zf2[:], 0.0, A.max, A.min, deps=(b_zf,), cross=True)
+    v("ts", T.r8i[:], T.ls[:, 15:128:16], TOP, None, A.mult, deps=("v", x_r8, s_r8, s_r9))
     v("ts", T.r8n[:], T.r8i[:], 127, None, A.bitwise_and)
     x_i0 = v("ts", i8(0), T.cs[:, 15:128:16], TOP, None, A.mult, deps=(x_cs,), cross=True)
     x_of = v("copy", T.offp[:], T.r8n[:], cross=True)
@@ -393,14 +431,8 @@ def rank_program(g, core, T, topo):
     s_x2 = op("s", "act", (T.x2s[:], T.win2s[:].indirect(T.ixu[:]), CP), (x_ix, "a2"))
     x_c2 = v("copy", T.cu2[:], f8(16), cross=True)
     x_x2 = v("copy", T.x2[:].bitcast(dt.uint32), T.win2[:].bitcast(dt.uint32).indirect(T.ixu[:]), deps=(x_ix, "a2"), cross=True)
-    rows = []
-
-    def between2():
-        v("copy", T.base2[:], T.sc2[:].indirect(T.cu2[:]), deps=("v", x_c2))
-        rows.append(v("copy", T.chr1[:], T.io1[:].indirect(T.cu1[:]), deps=(), cross=True))
-
-    update(T.hs2, T.h2, T.x2, T.x2s, T.e2t, ld_e2, (x_x2, s_x2), x_a, between2)
-    dma("y", T.ch[0:1, :], T.chr1[0:1, :], (rows[0],))
+    update(T.hs2, T.h2, T.x2, T.x2s, T.e2t, ld_e2, (x_x2, s_x2), x_a,
+           lambda: v("copy", T.base2[:], T.sc2[:].indirect(T.cu2[:]), deps=("v", x_c2)))
     x_h2 = v("quant", T.h2q[:], T.h2s[:], T.h2[:], cross=True)
     x_ch2 = v("copy", T.chr2[:], T.io1[:].indirect(T.cu2[:]), deps=(), cross=True)
 

from concourse.bass import DstId, RemoteDMATransfer
from concourse.mybir import dt, AluOpType, ActivationFunctionType

X4 = "float8_e4m3fn_x4"
F, B, I, U16, U8 = "float32", "bfloat16", "int32", "uint16", "uint8"


def _sb(n, d):
    return ("sbuf", [128, n], d)


SCRATCH = {
    "e0t": _sb(512, B), "e1t": _sb(512, B), "e2t": _sb(512, B), "at": _sb(2048, B), "wt": _sb(512, B), "ut": _sb(4, B),
    "ubig": _sb(512, B),
    "pst": ("dram", [128, 4], I), "pl": ("dram", [8, 128, 4], I),
    "l1": _sb(32, I), "lo": _sb(32, I), "l2": _sb(32, I),
    "uq": _sb(128, X4), "us": _sb(128, U8), "aq": _sb(512, X4), "asc": _sb(512, U8), "wq": _sb(128, X4), "ws": _sb(128, U8),
    "hall": _sb(1024, X4), "halls": _sb(1024, U8), "x1": _sb(128, X4), "x1s": _sb(128, U8),
    "h1q": _sb(128, X4), "h1s": _sb(128, U8), "pk": _sb(128, X4), "pks": _sb(128, U8),
    "win2": _sb(256, X4), "win2s": _sb(256, U8), "x2": _sb(128, X4), "x2s": _sb(128, U8),
    "h2q": _sb(128, X4), "h2s": _sb(128, U8),
    "ones": _sb(128, B), "hold32": _sb(512, B), "hold16": _sb(128, B), "rst": _sb(512, F), "pidx": _sb(1, I), "r15": _sb(1, I),
    "r31": _sb(1, I), "ip": _sb(1, F), "sp31": _sb(1, F), "spx": _sb(1, F), "spart": _sb(1, F), "cmod": _sb(128, I),
    "mask16": _sb(128, B), "ci": _sb(128, I), "repo": _sb(40, U16), "rsh": _sb(40, I), "dupo": _sb(16, U16),
    "io1": _sb(1024, F), "eidx": _sb(512, F),
    "off1": _sb(32, U16), "offo": _sb(32, U16), "offh": _sb(16, U16), "off2": _sb(32, U16), "er": _sb(512, F), "er2": _sb(512, F),
    "kt": _sb(512, F), "kp": _sb(256, F), "key1": _sb(256, F), "key2": _sb(512, F), "st1": _sb(256, F),
    "ew": _sb(128, F), "es": _sb(128, F), "ew2": _sb(128, F), "es2": _sb(128, F),
    "sc": _sb(1024, F), "gv": _sb(512, F), "mx": _sb(512, F), "pm": _sb(512, B), "st": _sb(512, F),
    "zb1": _sb(128, I), "zf1": _sb(128, F), "zi2": _sb(128, I), "zb2": _sb(128, I), "zrow": _sb(128, F), "zf2": _sb(128, F),
    "sj": _sb(128, I), "mk": _sb(128, B), "th": _sb(128, B), "cum": _sb(128, B), "cs": _sb(128, F),
    "dup1": _sb(256, B), "dup2": _sb(256, B), "v2": _sb(256, B), "vt": _sb(256, B), "vs": _sb(256, B),
    "f8": _sb(160, F), "i8": _sb(32, I), "cu1": _sb(8, U16), "cu2": _sb(8, U16),
    "base1": _sb(128, F), "bt": _sb(128, F), "gt": _sb(128, F), "sp": _sb(32, F), "d1": _sb(512, F), "rp": _sb(1024, F),
    "sc2": _sb(1024, F), "base2": _sb(128, F), "gout": _sb(128, F), "yt": _sb(128, F),
    "am": _sb(128, I), "mb": _sb(144, B), "ce": _sb(128, B), "pp": _sb(128, B), "ks": _sb(128, F), "lr": _sb(32, F),
    "lt": _sb(32, F), "ls": _sb(128, F), "r8i": _sb(8, I), "r8n": _sb(8, I), "offp": _sb(8, U16),
    "ixu": _sb(8, U16), "chr1": _sb(128, F), "chr2": _sb(128, F),
    "hs1": _sb(512, F), "hs2": _sb(512, F), "h1": _sb(512, B), "h2": _sb(512, B),
    "ps": ("psum", [128, 2048], F), "pr": ("psum", [128, 2048], F),
}

REMOTE = ["al", "a0a", "a0b", "a0h", "ae", "a2", "left", "hl", "hc", "kc", "ks"]
SEMAPHORES = REMOTE + ["v"] + ["s%d" % i for i in range(138)]
A = AluOpType
CP, IDN = ActivationFunctionType.Copy, ActivationFunctionType.Identity
TOP = 2.0 ** 19

TIERS = (("a0a", {1: 2, 2: 2, 3: 2, 4: 2}), ("a0b", {5: 4, 6: 4}))
TIER_H = ("a0h", {7: 8})
LISTS = ({1: 2, 2: 2, 3: 2, 4: 2}, {5: 2, 6: 2, 7: 4})
SCORES = {q: 1 for q in range(1, 8)}
PICKS, PICKS_H = {1: 2, 2: 2, 3: 4}, ({4: 4, 5: 4}, {6: 4, 7: 4})


def helpers(core, topo):
    return [c for c in topo.cores_of(core) if topo.die(c) != topo.die(core)][:len(LISTS)]


def fused(g, T, topo, core, parts):
    tr = []
    for c, e, sem, src, dst in parts:
        rid, pid = topo.addr(c, core)
        tr.append(RemoteDMATransfer(dst_ids=[DstId(rid=rid, pnc=pid)], dma_engine_mask=sum(1 << x for x in e), remote_sem=T.sem[sem],
                                    srcs=[src], dsts=[dst]))
    g.remote_dma_fused(tr, local_sem=T.sem.left)
    return sum(len(e) for c, e, sem, src, dst in parts)


def far(T, topo, core, me, share, sem, src, dst):
    parts, at = [], 0
    for q, n in share.items():
        d = (me + q) % len(T.cores)
        parts.append((T.cores[d], topo.engines(core, T.cores[d])[at:at + n], sem, src(q), dst(d)))
        at += n
    return parts


def inner(T, topo, core, me):
    away = topo.engines(core, T.cores[(me + 1) % len(T.cores)])
    return [x for x in topo.engines(core, helpers(core, topo)[0]) if x not in away]


def near(T, topo, core, me, sem, src, n=None):
    hp, e = helpers(core, topo), inner(T, topo, core, me)
    m = len(e) // len(hp)
    return [(c, e[m * i:m * i + (n or m)], sem, src(i), src(i)) for i, c in enumerate(hp)]


def columns0(T, me):
    mine = slice(128 * me, 128 * me + 128)
    return T.hall[:, mine].bitcast(dt.uint8), T.halls[:, mine]


def pick_calls(T, me):
    land = slice(16 * me, 16 * me + 16)
    return (("kc", lambda q: T.pk[:, 16 * q:16 * q + 16].bitcast(dt.uint8), lambda d: T.win2[:, land].bitcast(dt.uint8)),
            ("ks", lambda q: T.pks[:, 16 * q:16 * q + 16], lambda d: T.win2s[:, land]))


def helper_program(g, core, T, topo, me, k):
    N, own = len(T.cores), T.cores[me]
    g.wait_ge(T.sem.hl, 1)
    left = fused(g, T, topo, core, far(T, topo, core, me, LISTS[k], "al", lambda q: T.pst[:], lambda d: T.pl[(me - d) % N]))
    g.wait_ge(T.sem.hc, len(inner(T, topo, own, me)))
    piece = columns0(T, me)[k]
    left += fused(g, T, topo, core, far(T, topo, core, me, TIER_H[1], TIER_H[0], lambda q: piece, lambda d: piece))
    n = len(near(T, topo, own, me, "kc", lambda i: None)[k][1])
    for sem, src, dst in pick_calls(T, me):
        g.wait_ge(T.sem[sem], n)
        left += fused(g, T, topo, core, far(T, topo, core, me, PICKS_H[k], "a2", src, dst))
    g.wait_ge(T.sem.left, left)


def rank_program(g, core, T, topo):
    me = T.rank_of(core)
    if me is None:
        for r, c in enumerate(T.cores):
            if core in helpers(c, topo):
                helper_program(g, core, T, topo, r, helpers(c, topo).index(core))
        return
    N = len(T.cores)
    Q = {"g": g, "v": g.vector, "s": g.scalar, "t": g.tensor, "y": g.sync}
    total, seen, used = {"left": 0}, {}, [0]

    def wait(q, deps):
        for sem in deps:
            assert sem != "v" or q == "v"
            if seen.get((q, sem), 0) < total.get(sem, 0):
                Q[q].wait_ge(T.sem[sem], total[sem])
                seen[(q, sem)] = total[sem]

    def fresh():
        used[0] += 1
        return "s%d" % (used[0] - 1)

    def mark(q, ins, n, cross, sem=None):
        if sem is None:
            sem = "v" if q == "v" and not cross else fresh()
        total[sem] = total.get(sem, 0) + n
        ins.then_inc(T.sem[sem], n)
        return sem

    def dma(q, out, in_, deps=(), sem=None):
        wait(q, deps)
        return mark(q, Q[q].dma_start(out, in_), 16, True, sem)

    F_ = {"copy": g.vector.tensor_copy, "tt": g.vector.tensor_tensor, "ts": g.vector.tensor_scalar, "set": g.vector.memset,
          "scan": g.vector.tensor_tensor_scan, "tr": g.vector.transpose, "quant": g.vector.quantize_mx,
          "mm": g.tensor.matmul_mx, "act": g.scalar.activation, "iota": g.iota, "bc": g.partition_broadcast}

    def op(q, name, args, deps=(), cross=True, sem=None, **kw):
        wait(q, deps)
        return mark(q, F_[name](*args, **kw), 1, cross, sem)

    def v(name, *args, deps=("v",), cross=False, sem=None):
        return op("v", name, args, deps, cross, sem)

    def send(parts, deps):
        wait("g", deps)
        total["left"] += fused(g, T, topo, core, parts)

    def count(*shares):
        return sum(n for share in shares for n in share.values())

    total["al"], total["ae"], total["a2"] = count(*LISTS), count(SCORES), 2 * count(PICKS, *PICKS_H)
    for sem, share in TIERS + (TIER_H,):
        total[sem] = 2 * count(share)
    arrivals = [sem for sem, share in TIERS + (TIER_H,)]
    mine = slice(128 * me, 128 * me + 128)
    halves = slice(0, 64), slice(64, 128)
    two = {name: (fresh(), fresh()) for name in ("scan", "mark", "key", "whole", "rank")}

    ld_e0 = dma("y", T.e0t[:], T.e0[:])
    ld_ps = dma("s", T.pst[:], T.p2[:])
    ld_u = dma("s", T.ut[:], T.u[:, 0:4])
    ld_own = dma("s", T.pl[0], T.p2[:])
    ld_l1, ld_lo = None, None
    for k in range(8):
        ld_l1 = dma("y", T.l1[16 * k:16 * k + 16, :], T.p1[:], (), ld_l1)
    for k in range(8):
        ld_lo = dma("y", T.lo[16 * k:16 * k + 16, :], T.p2[:], (), ld_lo)
    wait("y", arrivals[:1])
    ld_a = dma("y", T.at[:], T.a[:])
    wait("y", arrivals)
    ld_e1 = dma("y", T.e1t[:], T.e1[:])
    ld_l2 = dma("y", T.l2[:], T.pl[:], ("al", ld_own))
    ld_w = dma("y", T.wt[:], T.w[:])
    ld_e2 = dma("y", T.e2t[:], T.e2[:])

    i_p = op("g", "iota", (T.pidx[:], [[0, 1]], 0, 1))
    i_0 = op("g", "iota", (T.io1[:, 0:128], [[1, 128]], 0, 0), allow_small_or_imprecise_dtypes=True)
    i_1 = fresh()
    for k in range(1, 8):
        op("s", "act", (T.io1[:, 128 * k:128 * k + 128], T.io1[:, 0:128], IDN), (i_0,), sem=i_1, bias=float(128 * k))

    send(near(T, topo, core, me, "hl", lambda i: T.pst[:], 1), (ld_ps,))
    x_h0 = v("quant", T.hall[:, mine], T.halls[:, mine], T.e0t[:], deps=(ld_e0,), cross=True)
    for sem, share in TIERS:
        if sem == TIERS[1][0]:
            for c, piece in zip(helpers(core, topo), columns0(T, me)):
                send([(c, inner(T, topo, core, me), "hc", piece, piece)], (x_h0,))
        for piece in columns0(T, me):
            send(far(T, topo, core, me, share, sem, lambda q: piece, lambda d: piece), (x_h0,))

    v("set", T.ones[:], 1.0)
    v("ts", T.r15[:], T.pidx[:], 15, None, A.bitwise_and, deps=(i_p,))
    v("ts", T.r31[:], T.pidx[:], 31, None, A.bitwise_and, deps=())
    v("copy", T.ci[:], T.io1[:, 0:128], deps=(i_0,))
    for buf, c in ((T.hold32[:, 0:256], 1.0), (T.hold16[:], 1.0), (T.rst[:, 0:256], 0.0), (T.pm[:, 0:512:4], 1.0), (T.mb[:, 0:1], 0.0)):
        v("set", buf, c, deps=())
    s_e = op("s", "act", (T.eidx[:], T.io1[:, 0:512], CP), (i_1,), scale=1024.0 / TOP)

    for a in range(2):
        v("copy", T.offh[64 * a:64 * a + 64, :], T.l1[64 * a:64 * a + 64, 16 * a:16 * a + 16], deps=(ld_l1,))
    v("copy", T.off1[:], T.l1[:], deps=())
    for t in range(4):
        v("ts", T.ubig[:, t:512:4], T.ones[:], T.ut[:, t:t + 1], None, A.mult, deps=("v", ld_u) if t == 0 else ())
    x_off1 = v("copy", T.ip[:], T.r15[:], cross=True)
    s_kp = op("s", "act", (T.kp[:], T.io1[:].indirect(T.offh[:]), CP), (x_off1, i_1), scale=1.0 / TOP)
    s_er = op("s", "act", (T.er[:], T.io1[:].indirect(T.off1[:]), CP))
    x_u = v("quant", T.uq[:], T.us[:], T.ubig[:], deps=("v",), cross=True)
    v("set", T.hold32[:, 0:256:32], 0.0, deps=())
    v("set", T.hold16[:, 0:128:16], 0.0, deps=())
    v("set", T.rst[:, 0:256:4], -1.0e29, deps=())
    v("copy", T.sp31[:], T.r31[:], deps=())
    v("ts", T.cmod[:], T.ci[:], 15, None, A.bitwise_and, deps=())
    v("ts", T.rsh[:], T.ci[:, 0:40], 1, None, A.logical_shift_right, deps=())
    v("ts", T.spx[:], T.sp31[:], float(me), 99.0, A.is_equal, A.mult, deps=("v", x_off1))
    v("ts", T.mask16[:], T.cmod[:], T.ip[:], None, A.is_equal, deps=())
    v("ts", T.dupo[:], T.rsh[:, 0:16], 16.0, T.ip[:], A.mult, A.add, deps=())
    x_rep = v("ts", T.repo[:], T.rsh[:], 12.0, None, A.add, deps=(), cross=True)
    v("tt", T.spart[:], T.spx[:], T.sp31[:], A.add)
    for a in range(2):
        h = slice(64 * a, 64 * a + 64)
        v("tt", T.key1[h, :], T.kp[h, :], T.eidx[h, 256 * a:256 * a + 256], A.add, deps=(s_kp, s_e))

    def e0table(ew, es, row, deps):
        v("tt", ew[:], row[:, 0:512:4], T.mask16[:], A.mult, deps=deps)
        v("scan", es[:], T.hold16[:], ew[:], 0.0, A.mult, A.add)

    x_offo = v("copy", T.offo[:], T.lo[:], deps=(ld_lo,), cross=True)
    s_er2 = op("s", "act", (T.er2[:], T.io1[:].indirect(T.offo[:]), CP), (x_offo,))
    e0table(T.ew, T.es, T.er, ("v", s_er))
    v("set", T.d1[:], 0.0, deps=())
    v("set", T.hold32[:, 256:512], 1.0, deps=())
    v("set", T.rst[:, 256:512], 0.0, deps=())
    v("set", T.hold32[:, 256:512:32], 0.0)
    v("set", T.rst[:, 256:512:4], -1.0e29, deps=())
    e0table(T.ew2, T.es2, T.er2, ("v", s_er2))

    sc_done = []
    order = [(me, x_h0)] + [((me - q) % N, sem) for sem, share in (TIERS[0], TIER_H, TIERS[1]) for q in share]
    for i, (r, sem) in enumerate(order):
        cs = slice(128 * r, 128 * r + 128)
        bank = (T.ps if i < 4 else T.pr)[:, 512 * (i % 4):512 * (i % 4) + 128]
        m = op("t", "mm", (bank, T.uq[:], T.us[:], T.hall[:, cs], T.halls[:, cs], True, True), (x_u, sem))
        if i % 2:
            sc_done.append(v("copy", T.sc[:, cs], bank, deps=(m,), cross=True))
        else:
            sc_done.append(op("s", "act", (T.sc[:, cs], bank, CP), (m,)))
    arrived = [x_h0] + arrivals

    def choose(w, parts, key, st):
        h = w // 2
        for i in range(2):
            c = slice(h * i, h * i + h)
            v("scan", T.mx[:, c], T.rst[:, c], T.gv[:, c], 0.0, A.add, A.max, deps=(parts[i],), sem=two["scan"][i])
        for i in range(2):
            for k in (1, 2, 3):
                a, e = h * i + k, h * i + h
                v("tt", T.pm[:, a:e:4], T.gv[:, a:e:4], T.mx[:, a - 1:e:4], A.is_gt, deps=(two["scan"][i],), sem=two["mark"][i])
        for i in range(2):
            c = slice(h * i, h * i + h)
            v("scan", st[:, c], T.pm[:, c], key[:, c], 0.0, A.max, A.min, deps=(two["mark"][i],), sem=two["key"][i])
        return two["key"]

    def f8(i):
        return T.f8[:, 8 * i:8 * i + 8]

    def i8(i):
        return T.i8[:, 8 * i:8 * i + 8]

    etab, etab2, cnt = T.es[:, 15:128:16], T.es2[:, 15:128:16], T.vs[:, 31:256:32]

    def quant_a(i):
        return v("quant", T.aq[:, 128 * i:128 * i + 128], T.asc[:, 128 * i:128 * i + 128], T.at[:, 512 * i:512 * i + 512], deps=(ld_a,),
                 cross=True)

    def update(hs, h, X, Xs, e, ld_e, deps, x_a, between=None):
        dep = []
        for i in range(4):
            s = slice(128 * i, 128 * i + 128)
            m = op("t", "mm", (T.pr[:, 512 * i:512 * i + 128], T.aq[:, s], T.asc[:, s], X[:], Xs[:], True, True), tuple(deps) + (x_a[i],))
            dep.append(op("s", "act", (hs[:, s], T.pr[:, 512 * i:512 * i + 128], CP), (m,), scale=0.05))
        if between:
            between()
        for i in range(4):
            v("tt", h[:, i:512:4], hs[:, 128 * i:128 * i + 128], e[:, i:512:4], A.add, deps=(dep[i], ld_e))

    x_g1 = v("copy", T.gv[:, 0:128], T.sc[:].indirect(T.offh[:, 0:8]), deps=["v"] + sc_done, cross=True)
    s_g1 = op("s", "act", (T.gv[:, 128:256], T.sc[:].indirect(T.offh[:, 8:16]), CP), sc_done)
    x_st1 = choose(256, (x_g1, s_g1), T.key1, T.st1)
    s_zf = fresh()
    for a, to in enumerate(halves):
        for there in halves:
            v("ts", T.zb1[there, to], T.st1[to, 3:256:4], TOP, None, A.mult, deps=x_st1, sem=two["whole"][a])
            op("s", "act", (T.zf1[there, to], T.st1[to, 3:256:4], CP), x_st1, sem=s_zf)

    for i, c in enumerate(halves):
        v("ts", T.sj[:, c], T.zb1[:, c], 7, 7, A.logical_shift_right, A.bitwise_and, deps=(two["whole"][i],), sem=two["rank"][i])
    x_th = fresh()
    for i, c in enumerate(halves):
        v("ts", T.th[:, c], T.sj[:, c], T.spart[:], 1.0e6, A.not_equal, A.mult, deps=(two["rank"][i],), sem=x_th)
    s_th = op("s", "act", (T.dup1[:], T.th[:].indirect(T.dupo[:]), CP), (x_th,))
    v("ts", T.mk[:], T.sj[:], T.spart[:], None, A.is_equal, deps=())
    x_cum1 = v("scan", T.cum[:], T.ones[:], T.mk[:], -16.5, A.mult, A.add, cross=True)
    x_cs1 = v("scan", T.cs[:], T.mask16[:], T.zf1[:], 0.0, A.max, A.min, deps=(s_zf,), cross=True)
    x_a = [quant_a(0)]
    x_v1 = v("tt", T.v2[:], T.cum[:].indirect(T.dupo[:]), T.dup1[:], A.is_gt, deps=(x_cum1, s_th), cross=True)
    x_i0 = v("ts", i8(0), T.cs[:, 15:128:16], TOP, None, A.mult, deps=(x_cs1,), cross=True)
    x_vt = v("tr", T.vt[:], T.v2[:], deps=(x_v1,), cross=True)
    x_i1 = v("ts", i8(1), i8(0), 1023, None, A.bitwise_and, deps=(x_i0,), cross=True)
    v("scan", T.vs[:], T.hold32[:, 0:256], T.vt[:], 0.0, A.mult, A.add, deps=(x_vt,))
    v("tt", f8(0), etab, i8(1), A.subtract, deps=(x_i1,))
    v("tt", f8(1), cnt, f8(0), A.mult)
    v("tt", f8(2), f8(1), i8(1), A.add)
    x_c1 = v("copy", T.cu1[:], f8(2), cross=True)

    s_x1 = op("s", "act", (T.x1s[:], T.halls[:].indirect(T.cu1[:]), CP), [x_c1] + arrived)
    s_b1 = op("s", "act", (T.base1[:], T.sc[:].indirect(T.cu1[:]), CP))
    x_x1 = v("copy", T.x1[:].bitcast(dt.uint32), T.hall[:].bitcast(dt.uint32).indirect(T.cu1[:]), deps=[x_c1] + arrived, cross=True)
    x_a += [quant_a(i) for i in (1, 2, 3)]
    update(T.hs1, T.h1, T.x1, T.x1s, T.e1t, ld_e1, (x_x1, s_x1), x_a)
    x_h1 = v("quant", T.h1q[:], T.h1s[:], T.h1[:], cross=True)

    m = op("t", "mm", (T.ps[:, 0:128], T.uq[:], T.us[:], T.h1q[:], T.h1s[:], True, True), (x_h1,))
    x_off2 = v("copy", T.off2[:], T.l2[:], deps=(ld_l2,), cross=True)
    s_kt = op("s", "act", (T.kt[:], T.io1[:].indirect(T.off2[:]), CP), (x_off2,), scale=1.0 / TOP)
    v("tr", T.bt[:], T.base1[:], deps=(s_b1,))
    v("tr", T.gt[:], T.ps[:, 0:128], deps=(m,))
    x_sp = v("tt", T.sp[:, 4 * me:4 * me + 4], T.gt[:, 0:128:32], T.bt[:, 0:128:32], A.add, cross=True)
    own_sp = T.sp[:, 4 * me:4 * me + 4]
    send(far(T, topo, core, me, SCORES, "ae", lambda q: own_sp, lambda d: own_sp), (x_sp,))

    v("quant", T.win2[:, 128:256], T.win2s[:, 128:256], T.h1[:], deps=())
    x_w = v("quant", T.wq[:], T.ws[:], T.wt[:], deps=(ld_w,), cross=True)
    v("tt", T.key2[:], T.kt[:], T.eidx[:], A.add, deps=(s_kt, s_e))
    x_ch1 = v("copy", T.chr1[:], T.io1[:].indirect(T.cu1[:]), deps=(x_c1, i_1), cross=True)
    dma("y", T.ch[0:1, :], T.chr1[0:1, :], (x_ch1,))

    v("copy", T.d1[:, 0:384:32], T.sp[:, 0:12], deps=("v", "ae", x_sp))
    s_rp = [op("s", "act", (T.rp[:, 384:640], T.sp[:].indirect(T.repo[:, 0:16]), CP), ("ae", x_sp, x_rep)),
            op("s", "act", (T.rp[:, 640:1024], T.sp[:].indirect(T.repo[:, 16:40]), CP))]
    parts = slice(0, 192), slice(192, 384)
    for i, c in enumerate(parts):
        v("scan", T.rp[:, c], T.hold32[:, c], T.d1[:, c], 0.0, A.mult, A.add, deps=("v",) if i == 0 else (), sem=two["scan"][i])
    for i, c in enumerate(parts):
        v("tr", T.sc2[:, c], T.rp[:, c], deps=(two["scan"][i],))
    v("tr", T.sc2[:, 384:640], T.rp[:, 384:640], deps=(s_rp[0],))
    x_s2 = v("tr", T.sc2[:, 640:1024], T.rp[:, 640:1024], deps=(s_rp[1],), cross=True)

    wait("v", ("v", x_s2))
    x_s3 = v("copy", T.gv[:, 0:256], T.sc2[:].indirect(T.off2[:, 0:16]), deps=(), cross=True)
    s_g2 = op("s", "act", (T.gv[:, 256:512], T.sc2[:].indirect(T.off2[:, 16:32]), CP), (x_s2,))
    x_st = choose(512, (x_s3, s_g2), T.key2, T.st)
    for i, c in enumerate(halves):
        v("ts", T.zi2[:, c], T.st[:, 256 * i + 3:256 * i + 256:4], TOP, None, A.mult, deps=(x_st[i],), sem=two["whole"][i])
    s_zr = op("s", "act", (T.zrow[0:1, :], T.st[0:1, 3:512:4], CP), x_st)
    b_z = op("g", "bc", (T.zb2[:], T.zi2[0:1, :], 128), two["whole"])
    b_zf = op("g", "bc", (T.zf2[:], T.zrow[0:1, :], 128), (s_zr,))
    for i, c in enumerate(halves):
        v("ts", T.am[:, c], T.zi2[:, c], 896, None, A.bitwise_and, deps=(two["whole"][i],), sem=two["rank"][i])
    for i, c in enumerate(halves):
        v("ts", T.mb[:, 64 * i + 1:64 * i + 65], T.am[:, c], float(128 * me), None, A.is_equal, deps=(two["rank"][i],))
    v("scan", T.ce[:], T.ones[:], T.mb[:, 0:128], 0.0, A.mult, A.add)
    v("ts", T.pp[:], T.ce[:], T.ip[:], None, A.is_le)
    v("scan", T.ks[:], T.pp[:], T.st[:, 3:512:4], 0.0, A.max, A.min)
    v("ts", T.lr[:], T.mask16[:, 0:32], T.ks[:, 127:128], None, A.mult)
    x_sj = v("ts", T.sj[:], T.zb2[:], 7, 7, A.logical_shift_right, A.bitwise_and, deps=(b_z,), cross=True)
    v("tr", T.lt[:], T.lr[:])
    x_mk = v("ts", T.mk[:], T.sj[:], T.spart[:], None, A.is_equal, deps=(x_sj,), cross=True)
    x_ls, x_r8, s_r8 = fresh(), fresh(), fresh()
    for a in range(4):
        qa = slice(32 * a, 32 * a + 32)
        v("scan", T.ls[qa, qa], T.hold16[qa, 0:32], T.lt[qa, :], 0.0, A.mult, A.add, deps=("v",) if a == 0 else (), sem=x_ls)
    x_cum = v("scan", T.cum[:], T.ones[:], T.mk[:], 0.0, A.mult, A.add, deps=(x_mk,), cross=True)
    for a, b in ((0, 1), (1, 0), (2, 3), (3, 2)):
        out, src = [T.ls[32 * c:32 * c + 32, 32 * a + 15:32 * a + 32:16] for c in (b, a)]
        if a < 2:
            v("copy", out, src, deps=(x_ls,), sem=x_r8)
        else:
            op("s", "act", (out, src, CP), (x_ls,), sem=s_r8)
    s_r9 = op("s", "act", (T.ls[64:128, 15:64:16], T.ls[0:64, 15:64:16], CP), (x_r8,))
    v("copy", T.ls[0:64, 79:128:16], T.ls[64:128, 79:128:16], deps=(s_r8,))
    s_mk = op("s", "act", (T.dup2[:], T.mk[:].indirect(T.dupo[:]), CP), (x_mk,))
    x_cs = v("scan", T.cs[:], T.mask16[:], T.zf2[:], 0.0, A.max, A.min, deps=(b_zf,), cross=True)
    v("ts", T.r8i[:], T.ls[:, 15:128:16], TOP, None, A.mult, deps=("v", x_r8, s_r8, s_r9))
    v("ts", T.r8n[:], T.r8i[:], 127, None, A.bitwise_and)
    x_i0 = v("ts", i8(0), T.cs[:, 15:128:16], TOP, None, A.mult, deps=(x_cs,), cross=True)
    x_of = v("copy", T.offp[:], T.r8n[:], cross=True)
    x_i2 = v("ts", i8(2), i8(0), 1023, None, A.bitwise_and, deps=(x_i0,), cross=True)
    s_pk = op("s", "act", (T.pks[:], T.h1s[:].indirect(T.offp[:]), CP), (x_of, x_h1))
    x_pk = v("copy", T.pk[:].bitcast(dt.uint32), T.h1q[:].bitcast(dt.uint32).indirect(T.offp[:]), deps=(x_of, x_h1), cross=True)

    runs = [slice(16 * min(share), 16 * max(share) + 16) for share in PICKS_H]
    send(near(T, topo, core, me, "kc", lambda i: T.pk[:, runs[i]].bitcast(dt.uint8)), (x_pk,))
    send(near(T, topo, core, me, "ks", lambda i: T.pks[:, runs[i]]), (s_pk,))
    for sem, src, dst in pick_calls(T, me):
        send(far(T, topo, core, me, PICKS, "a2", src, dst), ())

    base = float(128 - 128 * me)
    v("tt", T.v2[:], T.cum[:].indirect(T.dupo[:]), T.dup2[:], A.mult, deps=(x_cum, s_mk))
    v("ts", f8(4), i8(2), base, None, A.add, deps=(x_i2,))
    x_i3 = v("ts", i8(3), i8(2), 7, None, A.logical_shift_right, deps=(), cross=True)
    v("tr", T.vt[:], T.v2[:])
    v("tt", f8(5), etab2, i8(2), A.subtract, deps=())
    v("ts", f8(6), i8(3), 16.0, -1.0, A.mult, A.add, deps=(x_i3,))
    v("scan", T.vs[:], T.hold32[:, 0:256], T.vt[:], 0.0, A.mult, A.add)
    x_f7 = v("tt", f8(7), f8(6), f8(4), A.subtract, deps=(), cross=True)
    v("ts", f8(8), cnt, 16.5, None, A.is_gt)
    v("ts", f8(9), cnt, 0.5, None, A.is_gt, deps=())
    v("tt", f8(10), f8(7), cnt, A.add, deps=(x_f7,))
    v("tt", f8(12), f8(8), f8(5), A.mult)
    v("tt", f8(11), f8(9), f8(8), A.subtract, deps=())
    v("tt", f8(14), f8(12), f8(4), A.add)
    v("tt", f8(13), f8(11), f8(10), A.mult, deps=())
    v("tt", f8(15), f8(13), f8(14), A.add)
    x_ix = v("copy", T.ixu[:], f8(15), cross=True)
    v("tt", f8(16), f8(12), i8(2), A.add, deps=())
    s_x2 = op("s", "act", (T.x2s[:], T.win2s[:].indirect(T.ixu[:]), CP), (x_ix, "a2"))
    x_c2 = v("copy", T.cu2[:], f8(16), cross=True)
    x_x2 = v("copy", T.x2[:].bitcast(dt.uint32), T.win2[:].bitcast(dt.uint32).indirect(T.ixu[:]), deps=(x_ix, "a2"), cross=True)
    update(T.hs2, T.h2, T.x2, T.x2s, T.e2t, ld_e2, (x_x2, s_x2), x_a,
           lambda: v("copy", T.base2[:], T.sc2[:].indirect(T.cu2[:]), deps=("v", x_c2)))
    x_h2 = v("quant", T.h2q[:], T.h2s[:], T.h2[:], cross=True)
    x_ch2 = v("copy", T.chr2[:], T.io1[:].indirect(T.cu2[:]), deps=(), cross=True)

    m_y = op("t", "mm", (T.ps[:, 512:640], T.wq[:], T.ws[:], T.h2q[:], T.h2s[:], True, True), (x_h2, x_w))
    m_g = op("t", "mm", (T.ps[:, 0:128], T.uq[:], T.us[:], T.h2q[:], T.h2s[:], True, True), (x_h2,))
    dma("y", T.oc[:], T.h2q[:].bitcast(dt.uint8), (x_h2,))
    for k in range(4):
        dma("ys"[k // 2], T.osc[4 * k:4 * k + 4, :], T.h2s[32 * k:32 * k + 4, :], (x_h2,))
    dma("y", T.ch[1:2, :], T.chr2[0:1, :], (x_ch2,))
    s_y = op("s", "act", (T.yt[:], T.ps[:, 512:640], CP), (m_y,))
    x_g = v("tt", T.gout[:], T.ps[:, 0:128], T.base2[:], A.add, deps=("v", m_g), cross=True)
    dma("s", T.y[:], T.yt[:], (s_y,))
    dma("y", T["g"][:], T.gout[0:1, :], (x_g,))

    wait("v", ("v",))
    for sem in sorted(total):
        if sem != "v" and not any(seen.get((q, sem), 0) == total[sem] for q in Q):
            wait("g", (sem,))
